import numpy as np
import ml_dtypes


def mxq(x, axis, fmt="e4m3"):
    dtype, down = {"e4m3": (ml_dtypes.float8_e4m3fn, 7), "e5m2": (ml_dtypes.float8_e5m2, 14)}[fmt]
    v = np.moveaxis(np.asarray(x, np.float32).astype(ml_dtypes.bfloat16).astype(np.float64), axis, -1)
    blocks = v.reshape(v.shape[:-1] + (-1, 32))
    amax = np.abs(blocks).max(-1, keepdims=True)
    byte = np.maximum(np.where(amax > 0, np.frexp(amax)[1] - 1 + 127, 0) - down, 1)
    scale = np.exp2(byte - 127.0)
    codes = (blocks / scale).astype(np.float32).astype(dtype).astype(np.float64)
    return np.moveaxis((codes * scale).reshape(v.shape), -1, axis)


WIDE = False


def mx_kscale(k):
    if not WIDE:
        return np.ones(k)
    levels = np.array([10, -10, 5, -5, 0])
    if k % 512:
        return np.exp2(np.random.permutation(np.resize(levels, k // 32))).repeat(32)
    a = np.empty((k // 512, 16))
    for p in range(k // 512):
        a[p, :8] = np.random.permutation(np.resize(levels, 8))
        for g in range(8):
            far = levels[np.abs(levels - a[p, g]) >= 10]
            a[p, g + 8] = far[np.random.randint(len(far))]
    return np.exp2(a.ravel()).repeat(32)


def f64(x):
    return np.asarray(x).astype(np.float64)


def striped(idx):
    return np.tile(idx.reshape(-1, 16).T, (8, 1)).astype(np.uint16)


def unstriped(offs):
    return offs[:16].T.reshape(-1).astype(np.int64)

def planes(y):
    n, m = y.shape
    v = y.astype(np.float32).astype(ml_dtypes.bfloat16).astype(np.float64).reshape(n // 32, 32, m)
    top = np.abs(v).max(1)
    byte = np.clip(np.where(top > 0, np.frexp(top)[1] - 1 + 127 - 7, 1), 1, 254)
    codes = (v * np.exp2(127.0 - byte)[:, None, :]).reshape(n, m).astype(np.float32).astype(ml_dtypes.float8_e4m3fn).view(np.uint8)
    words = codes.reshape(n // 512, 128, 4, m).transpose(0, 1, 3, 2)
    return np.ascontiguousarray(words), np.ascontiguousarray(byte.astype(np.uint8).reshape(n // 512, 16, m))


K, T, S, N = 512, 1024, 512, 512
P = 2 ** 7


def setup_inputs():
    n = np.random.standard_normal
    s = mx_kscale(K)[:, None]
    return {
        "xT": (n((K, T)) * s).astype(np.float32),
        "gate": np.tile(np.random.uniform(0.2, 1.0, T), (P, 1)).astype(np.float32),
        "w1": (n((K, N)) / np.sqrt(K) / s).astype(np.float32),
        "offs": striped(np.random.permutation(T)[:S]),
    }


def reference(xT, gate, w1, offs):
    xq = mxq(f64(xT)[:, unstriped(offs)], 0, "e4m3")
    y = mxq(f64(w1), 0, "e4m3").T @ xq
    g = f64(gate)[:1][:, unstriped(offs)]
    out = np.zeros((N, T))
    out[:, unstriped(offs)] = y * g
    return (out,) + planes(out)

@@ -1,0 +1,166 @@
+from contextlib import ExitStack
+
+import concourse.mybir as mybir
+from concourse.masks import make_identity
+
+K, T, S, N = 512, 1024, 512, 512
+FLOPS = 2 * K * N * S
+
+F32 = mybir.dt.float32
+BF16 = mybir.dt.bfloat16
+U32 = mybir.dt.uint32
+I32 = mybir.dt.int32
+U16 = mybir.dt.uint16
+U8 = mybir.dt.uint8
+FP8X4 = mybir.dt.float8_e4m3fn_x4
+COPY = mybir.ActivationFunctionType.Copy
+MULT = mybir.AluOpType.mult
+
+P = 128
+PACK = 4
+LIST_ROWS = 16
+GATE_RUN = T // P
+W_SCALAR = 52
+WEAVE_SCALAR = 160
+HALF = T // 2
+CHUNK = 256
+
+
+def tile_picked_modgate_linnone_lo_kernel(tc, xT, gate, w1, offs, out_0, out_1, out_2):
+    nc = tc.nc
+    with ExitStack() as ctx:
+        keep = ctx.enter_context(tc.tile_pool(name="keep", bufs=1))
+        psum = ctx.enter_context(tc.psum_pool(name="psum", bufs=1))
+
+        offsets = keep.tile([P, S // LIST_ROWS], U16, name="offsets")
+        gate_runs = keep.tile([P, GATE_RUN], F32, name="gate_runs", tag="bf_slot1", align_bytes=64)
+        nc.sync.dma_start(gate_runs[:], gate[0, :].rearrange("(p e) -> p e", e=GATE_RUN))
+        x_rows = xT.rearrange("(p j) c -> p j c", j=PACK)
+        x_raw = [keep.tile([P, T], F32, name=f"x_raw{j}", tag=f"x_slot{j}", align_bytes=64) for j in range(PACK)]
+        for j in range(PACK):
+            nc.sync.dma_start(x_raw[j][:], x_rows[:, j, :])
+            if j == 0:
+                nc.sync.dma_start(offsets[:], offs)
+        w_raw = keep.tile([P, PACK, N], F32, name="w_raw", tag="w_slot", align_bytes=64)
+        nc.sync.dma_start(w_raw[:], w1.rearrange("(p j) c -> p j c", j=PACK))
+
+        warm_in = keep.tile([P, 1], F32, name="warm_in")
+        warm_out = keep.tile([P, 1], F32, name="warm_out")
+        nc.vector.memset(warm_in[:], 0.0)
+        nc.scalar.activation(warm_out[:], warm_in[:], COPY)
+
+        identity = keep.tile([P, P], F32, name="identity", tag="bf_slot0", align_bytes=64)
+        make_identity(nc, identity[:])
+        windows = [keep.tile([P, T], F32, name=f"window{t}", align_bytes=64) for t in range(PACK - 1)]
+        for t in range(PACK - 1):
+            nc.vector.memset(windows[t][:], 0.0)
+
+        gate_row = keep.tile([P, T], F32, name="gate_row", align_bytes=64)
+        gate_row_v = gate_row[:].rearrange("p (n e) -> p n e", e=GATE_RUN)
+        for b in range(GATE_RUN // PACK):
+            bank = psum.tile([P, PACK, P], F32, name=f"gate_bank{b}")
+            for i in range(PACK):
+                e = PACK * b + i
+                nc.tensor.transpose(bank[:, i, :], gate_runs[:, e : e + 1].to_broadcast([P, P]), identity[:])
+            nc.scalar.copy(gate_row_v[:, :, PACK * b : PACK * (b + 1)], bank[:].rearrange("p i n -> p n i"))
+
+        x_grouped = keep.tile([P, S, PACK], BF16, name="x_grouped", align_bytes=64)
+        for j in range(2):
+            x_bf = keep.tile([P, T], BF16, name=f"x_bf{j}", tag=f"bf_slot{j}", align_bytes=64)
+            nc.vector.tensor_copy(x_bf[:], x_raw[j][:])
+            nc.scalar.activation(x_grouped[:, :, j], x_bf[:].indirect(offsets[:]), COPY)
+        x_picked = keep.tile([P, 2, S], F32, name="x_picked", tag="x_slot1", align_bytes=64)
+        for j in range(2):
+            nc.vector.tensor_copy(x_picked[:, j, :], x_raw[2 + j][:].indirect(offsets[:]))
+        pairs = x_picked[:].rearrange("p j s -> p s j")
+        nc.vector.tensor_copy(x_grouped[:, WEAVE_SCALAR:, 2:], pairs[:, WEAVE_SCALAR:])
+        nc.scalar.copy(x_grouped[:, :WEAVE_SCALAR, 2:], pairs[:, :WEAVE_SCALAR])
+        x_codes = keep.tile([P, S], U32, name="x_codes", tag="last_window", align_bytes=64)
+        x_scales = keep.tile([P, S], U8, name="x_scales", align_bytes=64)
+        nc.vector.quantize_mx(
+            out=x_codes[:].bitcast(FP8X4), scales=x_scales[:], in_=x_grouped[:].rearrange("p s j -> p (s j)")
+        )
+
+        w_grouped = keep.tile([P, N * PACK], BF16, name="w_grouped", tag="x_slot1", align_bytes=64)
+        w_dst = w_grouped[:].rearrange("p (t m j) -> p m j t", t=PACK, j=PACK)
+        w_src = w_raw[:].rearrange("p j (m t) -> p m j t", t=PACK)
+        nc.scalar.copy(w_dst[:, :W_SCALAR], w_src[:, :W_SCALAR])
+        nc.vector.tensor_copy(w_dst[:, W_SCALAR:], w_src[:, W_SCALAR:])
+        w_codes = keep.tile([P, N], U32, name="w_codes", align_bytes=64)
+        w_scales = keep.tile([P, N], U8, name="w_scales", align_bytes=64)
+
+        def quantise_w(t0, t1):
+            nc.vector.quantize_mx(
+                out=w_codes[:, P * t0 : P * t1].bitcast(FP8X4),
+                scales=w_scales[:, P * t0 : P * t1],
+                in_=w_grouped[:, P * PACK * t0 : P * PACK * t1],
+            )
+
+        def product(acc, t, s0, s1):
+            nc.tensor.matmul_mx(
+                out=acc,
+                lhsT=w_codes[:, P * t : P * (t + 1)].bitcast(FP8X4),
+                lhsT_scale=w_scales[:, P * t : P * (t + 1)],
+                rhs=x_codes[:, s0:s1].bitcast(FP8X4),
+                rhs_scale=x_scales[:, s0:s1],
+                start=True,
+                stop=True,
+            )
+
+        y = [keep.tile([P, S], F32, name=f"y{t}", align_bytes=64) for t in range(PACK)]
+        quantise_w(0, 1)
+        gate_picked = keep.tile([P, S], F32, name="gate_picked", tag="w_slot", align_bytes=64)
+        nc.vector.tensor_copy(gate_picked[:], gate_row[:].indirect(offsets[:]))
+        quantise_w(1, 2)
+        quantise_w(2, 4)
+        for t in range(PACK):
+            acc = psum.tile([P, S], F32, name=f"acc{t}")
+            product(acc[:], t, 0, S)
+            nc.scalar.copy(y[t][:], acc[:])
+        windows.append(keep.tile([P, T], F32, name="window3", tag="last_window", align_bytes=64))
+        nc.gpsimd.memset(windows[PACK - 1][:], 0.0)
+
+        def scatter(t, s0, s1):
+            nc.vector.tensor_tensor(
+                windows[t][:].indirect(offsets[:, s0 // LIST_ROWS : s1 // LIST_ROWS]),
+                y[t][:, s0:s1],
+                gate_picked[:, s0:s1],
+                MULT,
+            )
+
+        out_rows = out_0.rearrange("(p t) c -> p t c", t=PACK)
+        grouped = [keep.tile([P, HALF, PACK], BF16, name=f"out_grouped{h}", align_bytes=64) for h in range(2)]
+        for t in range(PACK):
+            scatter(t, 0, S)
+            nc.sync.dma_start(out_rows[:, t, :], windows[t][:])
+            if t < 2:
+                for h in range(2):
+                    nc.scalar.copy(grouped[h][:, :, t], windows[t][:, HALF * h : HALF * (h + 1)])
+            elif t == 2:
+                nc.scalar.copy(grouped[0][:, :, 2:], windows[t][:, :HALF].unsqueeze(2).to_broadcast([P, HALF, 2]))
+                nc.scalar.copy(grouped[1][:, :, t], windows[t][:, HALF:])
+
+        last = PACK - 1
+        for c0 in range(0, HALF, CHUNK):
+            nc.scalar.copy(grouped[1][:, c0 : c0 + CHUNK, last], windows[last][:, HALF + c0 : HALF + c0 + CHUNK])
+        for c0 in range(0, HALF, CHUNK):
+            nc.vector.tensor_copy(grouped[0][:, c0 : c0 + CHUNK, last], windows[last][:, c0 : c0 + CHUNK])
+
+        out_codes = keep.tile([P, T], U32, name="out_codes", align_bytes=64)
+        out_scales = keep.tile([P, T], U8, name="out_scales", align_bytes=64)
+        words = out_1[0].rearrange("p c r -> p (c r)").bitcast(I32)
+        for h in range(2):
+            for c0 in range(0, HALF, CHUNK):
+                cols = slice(HALF * h + c0, HALF * h + c0 + CHUNK)
+                nc.vector.quantize_mx(
+                    out=out_codes[:, cols].bitcast(FP8X4),
+                    scales=out_scales[:, cols],
+                    in_=grouped[h][:, c0 : c0 + CHUNK, :].rearrange("p c t -> p (c t)"),
+                )
+            half = slice(HALF * h, HALF * (h + 1))
+            nc.sync.dma_start(words[:, half], out_codes[:, half].bitcast(I32))
+        for q in range(4):
+            queue = nc.sync if q < 2 else nc.scalar
+            queue.dma_start(
+                out_2[0, 4 * q : 4 * q + 4, :].bitcast(I32), out_scales[32 * q : 32 * q + 4, :].bitcast(I32)
+            )

@@ -15,15 +15,18 @@ U8 = mybir.dt.uint8
 FP8X4 = mybir.dt.float8_e4m3fn_x4
 COPY = mybir.ActivationFunctionType.Copy
 MULT = mybir.AluOpType.mult
+ADD = mybir.AluOpType.add
 
 P = 128
 PACK = 4
 LIST_ROWS = 16
 GATE_RUN = T // P
+FIRST = 128
 W_SCALAR = 52
-WEAVE_SCALAR = 160
-HALF = T // 2
-CHUNK = 256
+VECTOR_PIECES = ((0, 256), (256, 512))
+SCALAR_PIECES = ((512, 768), (768, 1024))
+QUANTISE_PIECES = ((0, 256), (256, 512), (512, 768), (768, 1024))
+STORE_AFTER = {512: 0, 768: 512, 1024: 768}
 
 
 def tile_picked_modgate_linnone_lo_kernel(tc, xT, gate, w1, offs, out_0, out_1, out_2):
@@ -33,7 +36,7 @@ def tile_picked_modgate_linnone_lo_kernel(tc, xT, gate, w1, offs, out_0, out_1, 
         psum = ctx.enter_context(tc.psum_pool(name="psum", bufs=1))
 
         offsets = keep.tile([P, S // LIST_ROWS], U16, name="offsets")
-        gate_runs = keep.tile([P, GATE_RUN], F32, name="gate_runs", tag="bf_slot1", align_bytes=64)
+        gate_runs = keep.tile([P, GATE_RUN], F32, name="gate_runs")
         nc.sync.dma_start(gate_runs[:], gate[0, :].rearrange("(p e) -> p e", e=GATE_RUN))
         x_rows = xT.rearrange("(p j) c -> p j c", j=PACK)
         x_raw = [keep.tile([P, T], F32, name=f"x_raw{j}", tag=f"x_slot{j}", align_bytes=64) for j in range(PACK)]
@@ -41,7 +44,7 @@ def tile_picked_modgate_linnone_lo_kernel(tc, xT, gate, w1, offs, out_0, out_1, 
             nc.sync.dma_start(x_raw[j][:], x_rows[:, j, :])
             if j == 0:
                 nc.sync.dma_start(offsets[:], offs)
-        w_raw = keep.tile([P, PACK, N], F32, name="w_raw", tag="w_slot", align_bytes=64)
+        w_raw = keep.tile([P, PACK, N], F32, name="w_raw", align_bytes=64)
         nc.sync.dma_start(w_raw[:], w1.rearrange("(p j) c -> p j c", j=PACK))
 
         warm_in = keep.tile([P, 1], F32, name="warm_in")
@@ -49,39 +52,45 @@ def tile_picked_modgate_linnone_lo_kernel(tc, xT, gate, w1, offs, out_0, out_1, 
         nc.vector.memset(warm_in[:], 0.0)
         nc.scalar.activation(warm_out[:], warm_in[:], COPY)
 
-        identity = keep.tile([P, P], F32, name="identity", tag="bf_slot0", align_bytes=64)
+        identity = keep.tile([P, P], F32, name="identity")
         make_identity(nc, identity[:])
-        windows = [keep.tile([P, T], F32, name=f"window{t}", align_bytes=64) for t in range(PACK - 1)]
-        for t in range(PACK - 1):
-            nc.vector.memset(windows[t][:], 0.0)
+        windows = [keep.tile([P, T], F32, name=f"window{t}", align_bytes=64) for t in range(PACK)]
+        for t in range(PACK):
+            engine = nc.vector if t < PACK - 1 else nc.gpsimd
+            engine.memset(windows[t][:], 0.0)
 
-        gate_row = keep.tile([P, T], F32, name="gate_row", align_bytes=64)
+        gate_row = keep.tile([P, T], F32, name="gate_row", tag="vector_stage", align_bytes=64)
         gate_row_v = gate_row[:].rearrange("p (n e) -> p n e", e=GATE_RUN)
         for b in range(GATE_RUN // PACK):
             bank = psum.tile([P, PACK, P], F32, name=f"gate_bank{b}")
             for i in range(PACK):
                 e = PACK * b + i
                 nc.tensor.transpose(bank[:, i, :], gate_runs[:, e : e + 1].to_broadcast([P, P]), identity[:])
-            nc.scalar.copy(gate_row_v[:, :, PACK * b : PACK * (b + 1)], bank[:].rearrange("p i n -> p n i"))
+            copy_out = nc.scalar.copy if b == 0 else nc.vector.tensor_copy
+            copy_out(gate_row_v[:, :, PACK * b : PACK * (b + 1)], bank[:].rearrange("p i n -> p n i"))
 
         x_grouped = keep.tile([P, S, PACK], BF16, name="x_grouped", align_bytes=64)
+        gate_picked = keep.tile([P, S], F32, name="gate_picked", align_bytes=64)
+        nc.vector.tensor_copy(gate_picked[:], gate_row[:].indirect(offsets[:]))
         for j in range(2):
-            x_bf = keep.tile([P, T], BF16, name=f"x_bf{j}", tag=f"bf_slot{j}", align_bytes=64)
-            nc.vector.tensor_copy(x_bf[:], x_raw[j][:])
+            x_bf = keep.tile([P, T], BF16, name=f"x_bf{j}", align_bytes=64)
+            nc.gpsimd.tensor_scalar(x_bf[:], x_raw[j][:], 1.0, 0.0, MULT, ADD)
             nc.scalar.activation(x_grouped[:, :, j], x_bf[:].indirect(offsets[:]), COPY)
-        x_picked = keep.tile([P, 2, S], F32, name="x_picked", tag="x_slot1", align_bytes=64)
+        x_picked = keep.tile([P, 2, S], F32, name="x_picked", tag="vector_stage", align_bytes=64)
         for j in range(2):
             nc.vector.tensor_copy(x_picked[:, j, :], x_raw[2 + j][:].indirect(offsets[:]))
-        pairs = x_picked[:].rearrange("p j s -> p s j")
-        nc.vector.tensor_copy(x_grouped[:, WEAVE_SCALAR:, 2:], pairs[:, WEAVE_SCALAR:])
-        nc.scalar.copy(x_grouped[:, :WEAVE_SCALAR, 2:], pairs[:, :WEAVE_SCALAR])
-        x_codes = keep.tile([P, S], U32, name="x_codes", tag="last_window", align_bytes=64)
+        nc.vector.tensor_copy(x_grouped[:, :, 2:], x_picked[:].rearrange("p j s -> p s j"))
+        x_codes = keep.tile([P, S], U32, name="x_codes", align_bytes=64)
         x_scales = keep.tile([P, S], U8, name="x_scales", align_bytes=64)
-        nc.vector.quantize_mx(
-            out=x_codes[:].bitcast(FP8X4), scales=x_scales[:], in_=x_grouped[:].rearrange("p s j -> p (s j)")
-        )
 
-        w_grouped = keep.tile([P, N * PACK], BF16, name="w_grouped", tag="x_slot1", align_bytes=64)
+        def quantise_x(s0, s1):
+            nc.vector.quantize_mx(
+                out=x_codes[:, s0:s1].bitcast(FP8X4),
+                scales=x_scales[:, s0:s1],
+                in_=x_grouped[:, s0:s1, :].rearrange("p s j -> p (s j)"),
+            )
+
+        w_grouped = keep.tile([P, N * PACK], BF16, name="w_grouped", tag="x_slot3", align_bytes=64)
         w_dst = w_grouped[:].rearrange("p (t m j) -> p m j t", t=PACK, j=PACK)
         w_src = w_raw[:].rearrange("p j (m t) -> p m j t", t=PACK)
         nc.scalar.copy(w_dst[:, :W_SCALAR], w_src[:, :W_SCALAR])
@@ -108,17 +117,23 @@ def tile_picked_modgate_linnone_lo_kernel(tc, xT, gate, w1, offs, out_0, out_1, 
             )
 
         y = [keep.tile([P, S], F32, name=f"y{t}", align_bytes=64) for t in range(PACK)]
+        quantise_x(0, FIRST)
         quantise_w(0, 1)
-        gate_picked = keep.tile([P, S], F32, name="gate_picked", tag="w_slot", align_bytes=64)
-        nc.vector.tensor_copy(gate_picked[:], gate_row[:].indirect(offsets[:]))
+        head = psum.tile([P, FIRST], F32, name="acc_head")
+        product(head[:], 0, 0, FIRST)
+        nc.scalar.copy(y[0][:, :FIRST], head[:])
+        quantise_x(FIRST, 2 * FIRST)
+        quantise_x(2 * FIRST, S)
+        rest = psum.tile([P, S - FIRST], F32, name="acc0")
+        product(rest[:, :FIRST], 0, FIRST, 2 * FIRST)
+        product(rest[:, FIRST:], 0, 2 * FIRST, S)
+        nc.scalar.copy(y[0][:, FIRST:], rest[:])
         quantise_w(1, 2)
         quantise_w(2, 4)
-        for t in range(PACK):
+        for t in range(1, PACK):
             acc = psum.tile([P, S], F32, name=f"acc{t}")
             product(acc[:], t, 0, S)
             nc.scalar.copy(y[t][:], acc[:])
-        windows.append(keep.tile([P, T], F32, name="window3", tag="last_window", align_bytes=64))
-        nc.gpsimd.memset(windows[PACK - 1][:], 0.0)
 
         def scatter(t, s0, s1):
             nc.vector.tensor_tensor(
@@ -129,38 +144,38 @@ def tile_picked_modgate_linnone_lo_kernel(tc, xT, gate, w1, offs, out_0, out_1, 
             )
 
         out_rows = out_0.rearrange("(p t) c -> p t c", t=PACK)
-        grouped = [keep.tile([P, HALF, PACK], BF16, name=f"out_grouped{h}", align_bytes=64) for h in range(2)]
-        for t in range(PACK):
-            scatter(t, 0, S)
-            nc.sync.dma_start(out_rows[:, t, :], windows[t][:])
-            if t < 2:
-                for h in range(2):
-                    nc.scalar.copy(grouped[h][:, :, t], windows[t][:, HALF * h : HALF * (h + 1)])
-            elif t == 2:
-                nc.scalar.copy(grouped[0][:, :, 2:], windows[t][:, :HALF].unsqueeze(2).to_broadcast([P, HALF, 2]))
-                nc.scalar.copy(grouped[1][:, :, t], windows[t][:, HALF:])
-
+        grouped = keep.tile([P, T, PACK], BF16, name="out_grouped", align_bytes=64)
         last = PACK - 1
-        for c0 in range(0, HALF, CHUNK):
-            nc.scalar.copy(grouped[1][:, c0 : c0 + CHUNK, last], windows[last][:, HALF + c0 : HALF + c0 + CHUNK])
-        for c0 in range(0, HALF, CHUNK):
-            nc.vector.tensor_copy(grouped[0][:, c0 : c0 + CHUNK, last], windows[last][:, c0 : c0 + CHUNK])
+        for t in range(PACK):
+            if t == 0:
+                scatter(t, 0, FIRST)
+                scatter(t, FIRST, S)
+            else:
+                scatter(t, 0, S)
+            nc.sync.dma_start(out_rows[:, t, :], windows[t][:])
+            if t < last - 1:
+                nc.scalar.copy(grouped[:, :, t], windows[t][:])
+            elif t == last - 1:
+                nc.scalar.copy(grouped[:, :, t:], windows[t][:].unsqueeze(2).to_broadcast([P, T, 2]))
+
+        for c0, c1 in SCALAR_PIECES:
+            nc.scalar.copy(grouped[:, c0:c1, last], windows[last][:, c0:c1])
+        for c0, c1 in VECTOR_PIECES:
+            nc.vector.tensor_copy(grouped[:, c0:c1, last], windows[last][:, c0:c1])
 
         out_codes = keep.tile([P, T], U32, name="out_codes", align_bytes=64)
         out_scales = keep.tile([P, T], U8, name="out_scales", align_bytes=64)
         words = out_1[0].rearrange("p c r -> p (c r)").bitcast(I32)
-        for h in range(2):
-            for c0 in range(0, HALF, CHUNK):
-                cols = slice(HALF * h + c0, HALF * h + c0 + CHUNK)
-                nc.vector.quantize_mx(
-                    out=out_codes[:, cols].bitcast(FP8X4),
-                    scales=out_scales[:, cols],
-                    in_=grouped[h][:, c0 : c0 + CHUNK, :].rearrange("p c t -> p (c t)"),
-                )
-            half = slice(HALF * h, HALF * (h + 1))
-            nc.sync.dma_start(words[:, half], out_codes[:, half].bitcast(I32))
+        for c0, c1 in QUANTISE_PIECES:
+            nc.vector.quantize_mx(
+                out=out_codes[:, c0:c1].bitcast(FP8X4),
+                scales=out_scales[:, c0:c1],
+                in_=grouped[:, c0:c1, :].rearrange("p c t -> p (c t)"),
+            )
+            if c1 in STORE_AFTER:
+                nc.sync.dma_start(words[:, STORE_AFTER[c1] : c1], out_codes[:, STORE_AFTER[c1] : c1].bitcast(I32))
         for q in range(4):
-            queue = nc.sync if q < 2 else nc.scalar
+            queue = nc.sync if q == 0 else nc.scalar
             queue.dma_start(
                 out_2[0, 4 * q : 4 * q + 4, :].bitcast(I32), out_scales[32 * q : 32 * q + 4, :].bitcast(I32)
             )

@@ -1,7 +1,6 @@
 from contextlib import ExitStack
 
 import concourse.mybir as mybir
-from concourse.masks import make_identity
 
 K, T, S, N = 512, 1024, 512, 512
 FLOPS = 2 * K * N * S
@@ -15,18 +14,14 @@ U8 = mybir.dt.uint8
 FP8X4 = mybir.dt.float8_e4m3fn_x4
 COPY = mybir.ActivationFunctionType.Copy
 MULT = mybir.AluOpType.mult
-ADD = mybir.AluOpType.add
 
 P = 128
 PACK = 4
+PAIR = 2
 LIST_ROWS = 16
-GATE_RUN = T // P
-FIRST = 128
-W_SCALAR = 52
-VECTOR_PIECES = ((0, 256), (256, 512))
-SCALAR_PIECES = ((512, 768), (768, 1024))
-QUANTISE_PIECES = ((0, 256), (256, 512), (512, 768), (768, 1024))
-STORE_AFTER = {512: 0, 768: 512, 1024: 768}
+HALF = T // 2
+W_SCALAR = 68
+CHUNK = 256
 
 
 def tile_picked_modgate_linnone_lo_kernel(tc, xT, gate, w1, offs, out_0, out_1, out_2):
@@ -36,8 +31,6 @@ def tile_picked_modgate_linnone_lo_kernel(tc, xT, gate, w1, offs, out_0, out_1, 
         psum = ctx.enter_context(tc.psum_pool(name="psum", bufs=1))
 
         offsets = keep.tile([P, S // LIST_ROWS], U16, name="offsets")
-        gate_runs = keep.tile([P, GATE_RUN], F32, name="gate_runs")
-        nc.sync.dma_start(gate_runs[:], gate[0, :].rearrange("(p e) -> p e", e=GATE_RUN))
         x_rows = xT.rearrange("(p j) c -> p j c", j=PACK)
         x_raw = [keep.tile([P, T], F32, name=f"x_raw{j}", tag=f"x_slot{j}", align_bytes=64) for j in range(PACK)]
         for j in range(PACK):
@@ -46,55 +39,42 @@ def tile_picked_modgate_linnone_lo_kernel(tc, xT, gate, w1, offs, out_0, out_1, 
                 nc.sync.dma_start(offsets[:], offs)
         w_raw = keep.tile([P, PACK, N], F32, name="w_raw", align_bytes=64)
         nc.sync.dma_start(w_raw[:], w1.rearrange("(p j) c -> p j c", j=PACK))
+        gate_row = keep.tile([P, T], F32, name="gate_row", align_bytes=64)
+        nc.sync.dma_start(gate_row[:], gate)
 
         warm_in = keep.tile([P, 1], F32, name="warm_in")
         warm_out = keep.tile([P, 1], F32, name="warm_out")
         nc.vector.memset(warm_in[:], 0.0)
         nc.scalar.activation(warm_out[:], warm_in[:], COPY)
 
-        identity = keep.tile([P, P], F32, name="identity")
-        make_identity(nc, identity[:])
         windows = [keep.tile([P, T], F32, name=f"window{t}", align_bytes=64) for t in range(PACK)]
         for t in range(PACK):
-            engine = nc.vector if t < PACK - 1 else nc.gpsimd
+            engine = nc.vector if t < PAIR else nc.gpsimd
             engine.memset(windows[t][:], 0.0)
 
-        gate_row = keep.tile([P, T], F32, name="gate_row", tag="vector_stage", align_bytes=64)
-        gate_row_v = gate_row[:].rearrange("p (n e) -> p n e", e=GATE_RUN)
-        for b in range(GATE_RUN // PACK):
-            bank = psum.tile([P, PACK, P], F32, name=f"gate_bank{b}")
-            for i in range(PACK):
-                e = PACK * b + i
-                nc.tensor.transpose(bank[:, i, :], gate_runs[:, e : e + 1].to_broadcast([P, P]), identity[:])
-            copy_out = nc.scalar.copy if b == 0 else nc.vector.tensor_copy
-            copy_out(gate_row_v[:, :, PACK * b : PACK * (b + 1)], bank[:].rearrange("p i n -> p n i"))
-
-        x_grouped = keep.tile([P, S, PACK], BF16, name="x_grouped", align_bytes=64)
-        gate_picked = keep.tile([P, S], F32, name="gate_picked", align_bytes=64)
-        nc.vector.tensor_copy(gate_picked[:], gate_row[:].indirect(offsets[:]))
-        for j in range(2):
+        x_grouped = keep.tile([P, S, PACK], BF16, name="x_grouped", tag="grouped_slot", align_bytes=64)
+        x_low = keep.tile([P, PAIR, S], BF16, name="x_low", align_bytes=64)
+        for j in range(PAIR):
             x_bf = keep.tile([P, T], BF16, name=f"x_bf{j}", align_bytes=64)
-            nc.gpsimd.tensor_scalar(x_bf[:], x_raw[j][:], 1.0, 0.0, MULT, ADD)
-            nc.scalar.activation(x_grouped[:, :, j], x_bf[:].indirect(offsets[:]), COPY)
-        x_picked = keep.tile([P, 2, S], F32, name="x_picked", tag="vector_stage", align_bytes=64)
-        for j in range(2):
-            nc.vector.tensor_copy(x_picked[:, j, :], x_raw[2 + j][:].indirect(offsets[:]))
-        nc.vector.tensor_copy(x_grouped[:, :, 2:], x_picked[:].rearrange("p j s -> p s j"))
-        x_codes = keep.tile([P, S], U32, name="x_codes", align_bytes=64)
-        x_scales = keep.tile([P, S], U8, name="x_scales", align_bytes=64)
-
-        def quantise_x(s0, s1):
-            nc.vector.quantize_mx(
-                out=x_codes[:, s0:s1].bitcast(FP8X4),
-                scales=x_scales[:, s0:s1],
-                in_=x_grouped[:, s0:s1, :].rearrange("p s j -> p (s j)"),
-            )
+            nc.vector.tensor_copy(x_bf[:], x_raw[j][:])
+            nc.scalar.activation(x_low[:, j, :], x_bf[:].indirect(offsets[:]), COPY)
+        nc.scalar.copy(x_grouped[:, :, :PAIR], x_low[:].rearrange("p j s -> p s j"))
+        x_high = keep.tile([P, PAIR, S], F32, name="x_high", align_bytes=64)
+        for j in range(PAIR):
+            nc.vector.tensor_copy(x_high[:, j, :], x_raw[PAIR + j][:].indirect(offsets[:]))
+        nc.vector.tensor_copy(x_grouped[:, :, PAIR:], x_high[:].rearrange("p j s -> p s j"))
 
         w_grouped = keep.tile([P, N * PACK], BF16, name="w_grouped", tag="x_slot3", align_bytes=64)
         w_dst = w_grouped[:].rearrange("p (t m j) -> p m j t", t=PACK, j=PACK)
         w_src = w_raw[:].rearrange("p j (m t) -> p m j t", t=PACK)
         nc.scalar.copy(w_dst[:, :W_SCALAR], w_src[:, :W_SCALAR])
         nc.vector.tensor_copy(w_dst[:, W_SCALAR:], w_src[:, W_SCALAR:])
+
+        x_codes = keep.tile([P, S], U32, name="x_codes", align_bytes=64)
+        x_scales = keep.tile([P, S], U8, name="x_scales", align_bytes=64)
+        nc.vector.quantize_mx(
+            out=x_codes[:].bitcast(FP8X4), scales=x_scales[:], in_=x_grouped[:].rearrange("p s j -> p (s j)")
+        )
         w_codes = keep.tile([P, N], U32, name="w_codes", align_bytes=64)
         w_scales = keep.tile([P, N], U8, name="w_scales", align_bytes=64)
 
@@ -105,75 +85,56 @@ def tile_picked_modgate_linnone_lo_kernel(tc, xT, gate, w1, offs, out_0, out_1, 
                 in_=w_grouped[:, P * PACK * t0 : P * PACK * t1],
             )
 
-        def product(acc, t, s0, s1):
+        quantise_w(0, 1)
+        gate_picked = keep.tile([P, S], F32, name="gate_picked", tag="grouped_slot", align_bytes=64)
+        nc.vector.tensor_copy(gate_picked[:], gate_row[:].indirect(offsets[:]))
+        quantise_w(1, 2)
+        quantise_w(2, 4)
+        y = [keep.tile([P, S], F32, name=f"y{t}", align_bytes=64) for t in range(PACK)]
+        for t in range(PACK):
+            acc = psum.tile([P, S], F32, name=f"acc{t}")
             nc.tensor.matmul_mx(
-                out=acc,
+                out=acc[:],
                 lhsT=w_codes[:, P * t : P * (t + 1)].bitcast(FP8X4),
                 lhsT_scale=w_scales[:, P * t : P * (t + 1)],
-                rhs=x_codes[:, s0:s1].bitcast(FP8X4),
-                rhs_scale=x_scales[:, s0:s1],
+                rhs=x_codes[:].bitcast(FP8X4),
+                rhs_scale=x_scales[:],
                 start=True,
                 stop=True,
             )
-
-        y = [keep.tile([P, S], F32, name=f"y{t}", align_bytes=64) for t in range(PACK)]
-        quantise_x(0, FIRST)
-        quantise_w(0, 1)
-        head = psum.tile([P, FIRST], F32, name="acc_head")
-        product(head[:], 0, 0, FIRST)
-        nc.scalar.copy(y[0][:, :FIRST], head[:])
-        quantise_x(FIRST, 2 * FIRST)
-        quantise_x(2 * FIRST, S)
-        rest = psum.tile([P, S - FIRST], F32, name="acc0")
-        product(rest[:, :FIRST], 0, FIRST, 2 * FIRST)
-        product(rest[:, FIRST:], 0, 2 * FIRST, S)
-        nc.scalar.copy(y[0][:, FIRST:], rest[:])
-        quantise_w(1, 2)
-        quantise_w(2, 4)
-        for t in range(1, PACK):
-            acc = psum.tile([P, S], F32, name=f"acc{t}")
-            product(acc[:], t, 0, S)
             nc.scalar.copy(y[t][:], acc[:])
-
-        def scatter(t, s0, s1):
-            nc.vector.tensor_tensor(
-                windows[t][:].indirect(offsets[:, s0 // LIST_ROWS : s1 // LIST_ROWS]),
-                y[t][:, s0:s1],
-                gate_picked[:, s0:s1],
-                MULT,
-            )
 
         out_rows = out_0.rearrange("(p t) c -> p t c", t=PACK)
         grouped = keep.tile([P, T, PACK], BF16, name="out_grouped", align_bytes=64)
         last = PACK - 1
         for t in range(PACK):
-            if t == 0:
-                scatter(t, 0, FIRST)
-                scatter(t, FIRST, S)
-            else:
-                scatter(t, 0, S)
+            nc.vector.tensor_tensor(windows[t][:].indirect(offsets[:]), y[t][:], gate_picked[:], MULT)
             nc.sync.dma_start(out_rows[:, t, :], windows[t][:])
             if t < last - 1:
                 nc.scalar.copy(grouped[:, :, t], windows[t][:])
             elif t == last - 1:
-                nc.scalar.copy(grouped[:, :, t:], windows[t][:].unsqueeze(2).to_broadcast([P, T, 2]))
+                nc.scalar.copy(grouped[:, :HALF, t:], windows[t][:, :HALF].unsqueeze(2).to_broadcast([P, HALF, PAIR]))
+                nc.scalar.copy(grouped[:, HALF:, t], windows[t][:, HALF:])
 
-        for c0, c1 in SCALAR_PIECES:
-            nc.scalar.copy(grouped[:, c0:c1, last], windows[last][:, c0:c1])
-        for c0, c1 in VECTOR_PIECES:
-            nc.vector.tensor_copy(grouped[:, c0:c1, last], windows[last][:, c0:c1])
+        for c0 in range(0, HALF, CHUNK):
+            nc.scalar.copy(grouped[:, HALF + c0 : HALF + c0 + CHUNK, last], windows[last][:, HALF + c0 : HALF + c0 + CHUNK])
+        for c0 in range(0, HALF, CHUNK):
+            nc.vector.tensor_copy(grouped[:, c0 : c0 + CHUNK, last], windows[last][:, c0 : c0 + CHUNK])
 
         out_codes = keep.tile([P, T], U32, name="out_codes", align_bytes=64)
         out_scales = keep.tile([P, T], U8, name="out_scales", align_bytes=64)
         words = out_1[0].rearrange("p c r -> p (c r)").bitcast(I32)
-        for c0, c1 in QUANTISE_PIECES:
+        stored = 0
+        for c0 in range(0, T, CHUNK):
+            c1 = c0 + CHUNK
             nc.vector.quantize_mx(
                 out=out_codes[:, c0:c1].bitcast(FP8X4),
                 scales=out_scales[:, c0:c1],
                 in_=grouped[:, c0:c1, :].rearrange("p c t -> p (c t)"),
             )
-            if c1 in STORE_AFTER:
-                nc.sync.dma_start(words[:, STORE_AFTER[c1] : c1], out_codes[:, STORE_AFTER[c1] : c1].bitcast(I32))
+            if c1 >= HALF:
+                nc.sync.dma_start(words[:, stored:c1], out_codes[:, stored:c1].bitcast(I32))
+                stored = c1
         for q in range(4):
             queue = nc.sync if q == 0 else nc.scalar
             queue.dma_start(

@@ -20,7 +20,7 @@ PACK = 4
 PAIR = 2
 LIST_ROWS = 16
 HALF = T // 2
-W_SCALAR = 68
+W_SCALAR = 64
 CHUNK = 256
 
 
@@ -32,12 +32,12 @@ def tile_picked_modgate_linnone_lo_kernel(tc, xT, gate, w1, offs, out_0, out_1, 
 
         offsets = keep.tile([P, S // LIST_ROWS], U16, name="offsets")
         x_rows = xT.rearrange("(p j) c -> p j c", j=PACK)
-        x_raw = [keep.tile([P, T], F32, name=f"x_raw{j}", tag=f"x_slot{j}", align_bytes=64) for j in range(PACK)]
+        x_raw = [keep.tile([P, T], F32, name=f"x_raw{j}", align_bytes=64) for j in range(PACK)]
         for j in range(PACK):
             nc.sync.dma_start(x_raw[j][:], x_rows[:, j, :])
             if j == 0:
                 nc.sync.dma_start(offsets[:], offs)
-        w_raw = keep.tile([P, PACK, N], F32, name="w_raw", align_bytes=64)
+        w_raw = keep.tile([P, PACK, N], F32, name="w_raw", tag="w_slot", align_bytes=64)
         nc.sync.dma_start(w_raw[:], w1.rearrange("(p j) c -> p j c", j=PACK))
         gate_row = keep.tile([P, T], F32, name="gate_row", align_bytes=64)
         nc.sync.dma_start(gate_row[:], gate)
@@ -52,21 +52,21 @@ def tile_picked_modgate_linnone_lo_kernel(tc, xT, gate, w1, offs, out_0, out_1, 
             engine = nc.vector if t < PAIR else nc.gpsimd
             engine.memset(windows[t][:], 0.0)
 
-        x_grouped = keep.tile([P, S, PACK], BF16, name="x_grouped", tag="grouped_slot", align_bytes=64)
-        x_low = keep.tile([P, PAIR, S], BF16, name="x_low", align_bytes=64)
+        x_grouped = keep.tile([P, S, PACK], BF16, name="x_grouped", align_bytes=64)
+        x_picked = keep.tile([P, PACK, S], BF16, name="x_picked", tag="stage_slot", align_bytes=64)
         for j in range(PAIR):
             x_bf = keep.tile([P, T], BF16, name=f"x_bf{j}", align_bytes=64)
             nc.vector.tensor_copy(x_bf[:], x_raw[j][:])
-            nc.scalar.activation(x_low[:, j, :], x_bf[:].indirect(offsets[:]), COPY)
-        nc.scalar.copy(x_grouped[:, :, :PAIR], x_low[:].rearrange("p j s -> p s j"))
-        x_high = keep.tile([P, PAIR, S], F32, name="x_high", align_bytes=64)
-        for j in range(PAIR):
-            nc.vector.tensor_copy(x_high[:, j, :], x_raw[PAIR + j][:].indirect(offsets[:]))
-        nc.vector.tensor_copy(x_grouped[:, :, PAIR:], x_high[:].rearrange("p j s -> p s j"))
+            nc.scalar.activation(x_picked[:, j, :], x_bf[:].indirect(offsets[:]), COPY)
+        for j in range(PAIR, PACK):
+            nc.vector.tensor_copy(x_picked[:, j, :], x_raw[j][:].indirect(offsets[:]))
+        by_entry = x_picked[:].rearrange("p j s -> p s j")
+        nc.scalar.copy(x_grouped[:, :, :PAIR], by_entry[:, :, :PAIR])
+        nc.vector.tensor_copy(x_grouped[:, :, PAIR:], by_entry[:, :, PAIR:])
 
-        w_grouped = keep.tile([P, N * PACK], BF16, name="w_grouped", tag="x_slot3", align_bytes=64)
-        w_dst = w_grouped[:].rearrange("p (t m j) -> p m j t", t=PACK, j=PACK)
-        w_src = w_raw[:].rearrange("p j (m t) -> p m j t", t=PACK)
+        w_grouped = keep.tile([P, N * PACK], BF16, name="w_grouped", tag="stage_slot", align_bytes=64)
+        w_dst = w_grouped[:].rearrange("p (t m j) -> p m t j", t=PACK, j=PACK)
+        w_src = w_raw[:].rearrange("p j (m t) -> p m t j", t=PACK)
         nc.scalar.copy(w_dst[:, :W_SCALAR], w_src[:, :W_SCALAR])
         nc.vector.tensor_copy(w_dst[:, W_SCALAR:], w_src[:, W_SCALAR:])
 
@@ -86,7 +86,7 @@ def tile_picked_modgate_linnone_lo_kernel(tc, xT, gate, w1, offs, out_0, out_1, 
             )
 
         quantise_w(0, 1)
-        gate_picked = keep.tile([P, S], F32, name="gate_picked", tag="grouped_slot", align_bytes=64)
+        gate_picked = keep.tile([P, S], F32, name="gate_picked", tag="w_slot", align_bytes=64)
         nc.vector.tensor_copy(gate_picked[:], gate_row[:].indirect(offsets[:]))
         quantise_w(1, 2)
         quantise_w(2, 4)

@@ -20,7 +20,7 @@ PACK = 4
 PAIR = 2
 LIST_ROWS = 16
 HALF = T // 2
-W_SCALAR = 64
+SH = S // 2
 CHUNK = 256
 
 
@@ -37,7 +37,7 @@ def tile_picked_modgate_linnone_lo_kernel(tc, xT, gate, w1, offs, out_0, out_1, 
             nc.sync.dma_start(x_raw[j][:], x_rows[:, j, :])
             if j == 0:
                 nc.sync.dma_start(offsets[:], offs)
-        w_raw = keep.tile([P, PACK, N], F32, name="w_raw", tag="w_slot", align_bytes=64)
+        w_raw = keep.tile([P, PACK, N], F32, name="w_raw", align_bytes=64)
         nc.sync.dma_start(w_raw[:], w1.rearrange("(p j) c -> p j c", j=PACK))
         gate_row = keep.tile([P, T], F32, name="gate_row", align_bytes=64)
         nc.sync.dma_start(gate_row[:], gate)
@@ -52,63 +52,85 @@ def tile_picked_modgate_linnone_lo_kernel(tc, xT, gate, w1, offs, out_0, out_1, 
             engine = nc.vector if t < PAIR else nc.gpsimd
             engine.memset(windows[t][:], 0.0)
 
-        x_grouped = keep.tile([P, S, PACK], BF16, name="x_grouped", align_bytes=64)
-        x_picked = keep.tile([P, PACK, S], BF16, name="x_picked", tag="stage_slot", align_bytes=64)
+        halves = [(h * SH, (h + 1) * SH) for h in range(2)]
+
+        def offs_of(s0, s1):
+            return offsets[:, s0 // LIST_ROWS : s1 // LIST_ROWS]
+
+        x_grouped = keep.tile([P, S * PACK], BF16, name="x_grouped", align_bytes=64)
+        woven = x_grouped[:].rearrange("p (s j) -> p s j", j=PACK)
         for j in range(PAIR):
             x_bf = keep.tile([P, T], BF16, name=f"x_bf{j}", align_bytes=64)
             nc.vector.tensor_copy(x_bf[:], x_raw[j][:])
-            nc.scalar.activation(x_picked[:, j, :], x_bf[:].indirect(offsets[:]), COPY)
-        for j in range(PAIR, PACK):
-            nc.vector.tensor_copy(x_picked[:, j, :], x_raw[j][:].indirect(offsets[:]))
-        by_entry = x_picked[:].rearrange("p j s -> p s j")
-        nc.scalar.copy(x_grouped[:, :, :PAIR], by_entry[:, :, :PAIR])
-        nc.vector.tensor_copy(x_grouped[:, :, PAIR:], by_entry[:, :, PAIR:])
-
-        w_grouped = keep.tile([P, N * PACK], BF16, name="w_grouped", tag="stage_slot", align_bytes=64)
-        w_dst = w_grouped[:].rearrange("p (t m j) -> p m t j", t=PACK, j=PACK)
-        w_src = w_raw[:].rearrange("p j (m t) -> p m t j", t=PACK)
-        nc.scalar.copy(w_dst[:, :W_SCALAR], w_src[:, :W_SCALAR])
-        nc.vector.tensor_copy(w_dst[:, W_SCALAR:], w_src[:, W_SCALAR:])
+            nc.scalar.activation(woven[:, :, j], x_bf[:].indirect(offsets[:]), COPY)
 
         x_codes = keep.tile([P, S], U32, name="x_codes", align_bytes=64)
         x_scales = keep.tile([P, S], U8, name="x_scales", align_bytes=64)
-        nc.vector.quantize_mx(
-            out=x_codes[:].bitcast(FP8X4), scales=x_scales[:], in_=x_grouped[:].rearrange("p s j -> p (s j)")
-        )
+        x_picked = keep.tile([P, PAIR * S], BF16, name="x_picked", align_bytes=64)
+        planes = x_picked[:].rearrange("p (j s) -> p j s", j=PAIR)
+        by_entry = x_picked[:].rearrange("p (j s) -> p s j", j=PAIR)
+        nc.vector.tensor_copy(planes[:, 0, :], x_raw[2][:].indirect(offsets[:]))
+        for s0, s1 in halves:
+            nc.vector.tensor_copy(planes[:, 1, s0:s1], x_raw[3][:].indirect(offs_of(s0, s1)))
+        nc.scalar.copy(woven[:, :SH, PAIR:], by_entry[:, :SH, :])
+        nc.vector.tensor_copy(woven[:, SH:, PAIR:], by_entry[:, SH:, :])
+        for s0, s1 in halves:
+            nc.vector.quantize_mx(
+                out=x_codes[:, s0:s1].bitcast(FP8X4), scales=x_scales[:, s0:s1], in_=x_grouped[:, PACK * s0 : PACK * s1]
+            )
+
+        shared = keep.tile([P, SH + S], F32, name="shared", align_bytes=64)
+        gate_picked = shared[:, :S]
+        late_grouped = keep.tile([P, PAIR * P * PACK], BF16, name="late_grouped", align_bytes=64)
+        w_grouped = [shared[:, SH:].bitcast(BF16), late_grouped[:]]
+        w_src = w_raw[:].rearrange("p j (m t) -> p m j t", t=PACK)
+        for h in range(2):
+            nc.scalar.copy(
+                w_grouped[h].rearrange("p (t m j) -> p m j t", t=PAIR, j=PACK), w_src[:, :, :, PAIR * h : PAIR * (h + 1)]
+            )
+
         w_codes = keep.tile([P, N], U32, name="w_codes", align_bytes=64)
         w_scales = keep.tile([P, N], U8, name="w_scales", align_bytes=64)
 
         def quantise_w(t0, t1):
+            h, first = divmod(t0, PAIR)
             nc.vector.quantize_mx(
                 out=w_codes[:, P * t0 : P * t1].bitcast(FP8X4),
                 scales=w_scales[:, P * t0 : P * t1],
-                in_=w_grouped[:, P * PACK * t0 : P * PACK * t1],
+                in_=w_grouped[h][:, PACK * P * first : PACK * P * (first + t1 - t0)],
             )
 
+        def pick_gate(s0, s1):
+            nc.vector.tensor_copy(gate_picked[:, s0:s1], gate_row[:].indirect(offs_of(s0, s1)))
+
+        pick_gate(*halves[0])
         quantise_w(0, 1)
-        gate_picked = keep.tile([P, S], F32, name="gate_picked", tag="w_slot", align_bytes=64)
-        nc.vector.tensor_copy(gate_picked[:], gate_row[:].indirect(offsets[:]))
         quantise_w(1, 2)
+        pick_gate(*halves[1])
         quantise_w(2, 4)
+
         y = [keep.tile([P, S], F32, name=f"y{t}", align_bytes=64) for t in range(PACK)]
-        for t in range(PACK):
-            acc = psum.tile([P, S], F32, name=f"acc{t}")
-            nc.tensor.matmul_mx(
-                out=acc[:],
-                lhsT=w_codes[:, P * t : P * (t + 1)].bitcast(FP8X4),
-                lhsT_scale=w_scales[:, P * t : P * (t + 1)],
-                rhs=x_codes[:].bitcast(FP8X4),
-                rhs_scale=x_scales[:],
-                start=True,
-                stop=True,
-            )
-            nc.scalar.copy(y[t][:], acc[:])
+        order = [0, 1, 2, 3]
+        pieces = {t: halves if t == order[0] else [(0, S)] for t in order}
+        for t in order:
+            for s0, s1 in pieces[t]:
+                acc = psum.tile([P, s1 - s0], F32, name=f"acc{t}_{s0}")
+                nc.tensor.matmul_mx(
+                    out=acc[:],
+                    lhsT=w_codes[:, P * t : P * (t + 1)].bitcast(FP8X4),
+                    lhsT_scale=w_scales[:, P * t : P * (t + 1)],
+                    rhs=x_codes[:, s0:s1].bitcast(FP8X4),
+                    rhs_scale=x_scales[:, s0:s1],
+                    start=True,
+                    stop=True,
+                )
+                nc.scalar.copy(y[t][:, s0:s1], acc[:])
 
         out_rows = out_0.rearrange("(p t) c -> p t c", t=PACK)
         grouped = keep.tile([P, T, PACK], BF16, name="out_grouped", align_bytes=64)
         last = PACK - 1
-        for t in range(PACK):
-            nc.vector.tensor_tensor(windows[t][:].indirect(offsets[:]), y[t][:], gate_picked[:], MULT)
+        for t in order:
+            nc.vector.tensor_tensor(windows[t][:].indirect(offsets[:]), y[t][:], gate_picked, MULT)
             nc.sync.dma_start(out_rows[:, t, :], windows[t][:])
             if t < last - 1:
                 nc.scalar.copy(grouped[:, :, t], windows[t][:])

@@ -1,6 +1,7 @@
 from contextlib import ExitStack
 
 import concourse.mybir as mybir
+from concourse.masks import make_identity
 
 K, T, S, N = 512, 1024, 512, 512
 FLOPS = 2 * K * N * S
@@ -22,6 +23,7 @@ LIST_ROWS = 16
 HALF = T // 2
 SH = S // 2
 CHUNK = 256
+LAST = P - 1
 
 
 def tile_picked_modgate_linnone_lo_kernel(tc, xT, gate, w1, offs, out_0, out_1, out_2):
@@ -30,88 +32,106 @@ def tile_picked_modgate_linnone_lo_kernel(tc, xT, gate, w1, offs, out_0, out_1, 
         keep = ctx.enter_context(tc.tile_pool(name="keep", bufs=1))
         psum = ctx.enter_context(tc.psum_pool(name="psum", bufs=1))
 
+        stage = ctx.enter_context(tc.tile_pool(name="stage", bufs=1))
+        gate_row = stage.tile([P, T], F32, name="gate_row", align_bytes=64, offset=0)
+        nc.gpsimd.memset(gate_row[:LAST, :], 0.0)
         offsets = keep.tile([P, S // LIST_ROWS], U16, name="offsets")
         x_rows = xT.rearrange("(p j) c -> p j c", j=PACK)
-        x_raw = [keep.tile([P, T], F32, name=f"x_raw{j}", align_bytes=64) for j in range(PACK)]
-        for j in range(PACK):
+        x_raw = {j: keep.tile([P, T], F32, name=f"x_raw{j}", align_bytes=64) for j in range(1, PACK)}
+        x_first = [keep.tile([P, HALF], F32, name=f"x_first{h}", align_bytes=64) for h in range(2)]
+        for h in range(2):
+            nc.sync.dma_start(x_first[h][:], x_rows[:, 0, HALF * h : HALF * (h + 1)])
+        nc.sync.dma_start(offsets[:], offs)
+        nc.sync.dma_start(gate_row[LAST:, :], gate[0:1, :])
+        for j in range(1, PACK):
             nc.sync.dma_start(x_raw[j][:], x_rows[:, j, :])
-            if j == 0:
-                nc.sync.dma_start(offsets[:], offs)
         w_raw = keep.tile([P, PACK, N], F32, name="w_raw", align_bytes=64)
         nc.sync.dma_start(w_raw[:], w1.rearrange("(p j) c -> p j c", j=PACK))
-        gate_row = keep.tile([P, T], F32, name="gate_row", align_bytes=64)
-        nc.sync.dma_start(gate_row[:], gate)
 
         warm_in = keep.tile([P, 1], F32, name="warm_in")
         warm_out = keep.tile([P, 1], F32, name="warm_out")
         nc.vector.memset(warm_in[:], 0.0)
         nc.scalar.activation(warm_out[:], warm_in[:], COPY)
 
-        windows = [keep.tile([P, T], F32, name=f"window{t}", align_bytes=64) for t in range(PACK)]
-        for t in range(PACK):
-            engine = nc.vector if t < PAIR else nc.gpsimd
-            engine.memset(windows[t][:], 0.0)
+        identity = keep.tile([P, P], F32, name="identity")
+        make_identity(nc, identity[:])
+        windows = [keep.tile([P, T], F32, name=f"window{t}", align_bytes=64) for t in range(PAIR)]
+        for t in range(PAIR):
+            nc.vector.memset(windows[t][:], 0.0)
 
         halves = [(h * SH, (h + 1) * SH) for h in range(2)]
 
         def offs_of(s0, s1):
             return offsets[:, s0 // LIST_ROWS : s1 // LIST_ROWS]
 
+        gate_first = keep.tile([P, S], F32, name="gate_first", align_bytes=64)
+
         x_grouped = keep.tile([P, S * PACK], BF16, name="x_grouped", align_bytes=64)
         woven = x_grouped[:].rearrange("p (s j) -> p s j", j=PACK)
         for j in range(PAIR):
             x_bf = keep.tile([P, T], BF16, name=f"x_bf{j}", align_bytes=64)
-            nc.vector.tensor_copy(x_bf[:], x_raw[j][:])
+            if j == 1:
+                nc.vector.tensor_copy(x_bf[:], x_raw[j][:])
+            else:
+                for h in range(2):
+                    nc.vector.tensor_copy(x_bf[:, HALF * h : HALF * (h + 1)], x_first[h][:])
+                nc.vector.tensor_copy(gate_first[:], gate_row[:].indirect(offsets[:]))
             nc.scalar.activation(woven[:, :, j], x_bf[:].indirect(offsets[:]), COPY)
+
+        blocks = S // P
+        gate_column = keep.tile([P, blocks], F32, name="gate_column")
+        nc.sync.dma_start(gate_column[:], gate_first[LAST:, :].rearrange("o (n b) -> o n b", b=blocks))
+        spread = psum.tile([P, blocks, P], F32, name="spread")
+        for b in range(blocks):
+            nc.tensor.transpose(spread[:, b, :], gate_column[:, b : b + 1].to_broadcast([P, P]), identity[:])
+        shared = stage.tile([P, PAIR * S + 2 * SH], BF16, name="shared", align_bytes=64, offset=0)
+        x_picked = shared[:, SH : SH + PAIR * S]
 
         x_codes = keep.tile([P, S], U32, name="x_codes", align_bytes=64)
         x_scales = keep.tile([P, S], U8, name="x_scales", align_bytes=64)
-        x_picked = keep.tile([P, PAIR * S], BF16, name="x_picked", align_bytes=64)
-        planes = x_picked[:].rearrange("p (j s) -> p j s", j=PAIR)
-        by_entry = x_picked[:].rearrange("p (j s) -> p s j", j=PAIR)
+        planes = x_picked.rearrange("p (j s) -> p j s", j=PAIR)
+        by_entry = x_picked.rearrange("p (j s) -> p s j", j=PAIR)
         nc.vector.tensor_copy(planes[:, 0, :], x_raw[2][:].indirect(offsets[:]))
-        for s0, s1 in halves:
+        for s0, s1 in reversed(halves):
             nc.vector.tensor_copy(planes[:, 1, s0:s1], x_raw[3][:].indirect(offs_of(s0, s1)))
-        nc.scalar.copy(woven[:, :SH, PAIR:], by_entry[:, :SH, :])
-        nc.vector.tensor_copy(woven[:, SH:, PAIR:], by_entry[:, SH:, :])
-        for s0, s1 in halves:
+        nc.scalar.copy(woven[:, SH:, PAIR:], by_entry[:, SH:, :])
+        nc.vector.tensor_copy(woven[:, :SH, PAIR:], by_entry[:, :SH, :])
+
+        def quantise_x(s0, s1):
             nc.vector.quantize_mx(
                 out=x_codes[:, s0:s1].bitcast(FP8X4), scales=x_scales[:, s0:s1], in_=x_grouped[:, PACK * s0 : PACK * s1]
             )
 
-        shared = keep.tile([P, SH + S], F32, name="shared", align_bytes=64)
-        gate_picked = shared[:, :S]
-        late_grouped = keep.tile([P, PAIR * P * PACK], BF16, name="late_grouped", align_bytes=64)
-        w_grouped = [shared[:, SH:].bitcast(BF16), late_grouped[:]]
         w_src = w_raw[:].rearrange("p j (m t) -> p m j t", t=PACK)
-        for h in range(2):
-            nc.scalar.copy(
-                w_grouped[h].rearrange("p (t m j) -> p m j t", t=PAIR, j=PACK), w_src[:, :, :, PAIR * h : PAIR * (h + 1)]
-            )
+        MH = P // 2
+        w_early = [shared[:, c0 : c0 + S].rearrange("p (t c) -> p t c", t=PAIR) for c0 in (PAIR * S, 0)]
+        w_late = stage.tile([P, PAIR, P * PACK], BF16, name="w_late", align_bytes=64, offset=7168)
+        quantise_x(*halves[1])
+        nc.scalar.copy(w_early[0].rearrange("p t (m j) -> p m j t", j=PACK), w_src[:, :MH, :, :PAIR])
+        nc.vector.tensor_copy(w_early[1].rearrange("p t (m j) -> p m j t", j=PACK), w_src[:, MH:, :, :PAIR])
+        quantise_x(*halves[0])
+        nc.scalar.copy(w_late[:].rearrange("p t (m j) -> p m j t", j=PACK), w_src[:, :, :, PAIR:])
 
         w_codes = keep.tile([P, N], U32, name="w_codes", align_bytes=64)
         w_scales = keep.tile([P, N], U8, name="w_scales", align_bytes=64)
 
-        def quantise_w(t0, t1):
-            h, first = divmod(t0, PAIR)
-            nc.vector.quantize_mx(
-                out=w_codes[:, P * t0 : P * t1].bitcast(FP8X4),
-                scales=w_scales[:, P * t0 : P * t1],
-                in_=w_grouped[h][:, PACK * P * first : PACK * P * (first + t1 - t0)],
-            )
+        def quantise_w(c0, c1, grouped_w):
+            nc.vector.quantize_mx(out=w_codes[:, c0:c1].bitcast(FP8X4), scales=w_scales[:, c0:c1], in_=grouped_w)
 
-        def pick_gate(s0, s1):
-            nc.vector.tensor_copy(gate_picked[:, s0:s1], gate_row[:].indirect(offs_of(s0, s1)))
+        for t in range(PAIR):
+            for h in reversed(range(2)):
+                quantise_w(P * t + MH * h, P * t + MH * (h + 1), w_early[h][:, t, :])
+        gate_picked = stage.tile([P, S], F32, name="gate_picked", align_bytes=64, offset=1024)
+        nc.vector.tensor_copy(gate_picked[:].rearrange("p (n b) -> p n b", b=blocks), spread[:].rearrange("p b n -> p n b"))
+        quantise_w(P * PAIR, N, w_late[:].rearrange("p t c -> p (t c)"))
 
-        pick_gate(*halves[0])
-        quantise_w(0, 1)
-        quantise_w(1, 2)
-        pick_gate(*halves[1])
-        quantise_w(2, 4)
+        for t in range(PAIR, PACK):
+            windows.append(stage.tile([P, T], F32, name=f"window{t}", align_bytes=64, offset=4096 * (t - 1)))
+            nc.gpsimd.memset(windows[t][:], 0.0)
 
         y = [keep.tile([P, S], F32, name=f"y{t}", align_bytes=64) for t in range(PACK)]
         order = [0, 1, 2, 3]
-        pieces = {t: halves if t == order[0] else [(0, S)] for t in order}
+        pieces = {t: halves[::-1] if t == order[0] else [(0, S)] for t in order}
         for t in order:
             for s0, s1 in pieces[t]:
                 acc = psum.tile([P, s1 - s0], F32, name=f"acc{t}_{s0}")
@@ -130,7 +150,7 @@ def tile_picked_modgate_linnone_lo_kernel(tc, xT, gate, w1, offs, out_0, out_1, 
         grouped = keep.tile([P, T, PACK], BF16, name="out_grouped", align_bytes=64)
         last = PACK - 1
         for t in order:
-            nc.vector.tensor_tensor(windows[t][:].indirect(offsets[:]), y[t][:], gate_picked, MULT)
+            nc.vector.tensor_tensor(windows[t][:].indirect(offsets[:]), y[t][:], gate_picked[:], MULT)
             nc.sync.dma_start(out_rows[:, t, :], windows[t][:])
             if t < last - 1:
                 nc.scalar.copy(grouped[:, :, t], windows[t][:])

@@ -23,6 +23,7 @@ LIST_ROWS = 16
 HALF = T // 2
 SH = S // 2
 CHUNK = 256
+FILL = 128
 LAST = P - 1
 
 
@@ -79,13 +80,14 @@ def tile_picked_modgate_linnone_lo_kernel(tc, xT, gate, w1, offs, out_0, out_1, 
             nc.scalar.activation(woven[:, :, j], x_bf[:].indirect(offsets[:]), COPY)
 
         blocks = S // P
-        gate_column = keep.tile([P, blocks], F32, name="gate_column")
-        nc.sync.dma_start(gate_column[:], gate_first[LAST:, :].rearrange("o (n b) -> o n b", b=blocks))
+        gate_column = keep.tile([P, blocks], F32, name="gate_column", tag="column_then_codes", align_bytes=64)
+        nc.gpsimd.dma_start(gate_column[:], gate_first[LAST:, :].rearrange("o (n b) -> o n b", b=blocks))
         spread = psum.tile([P, blocks, P], F32, name="spread")
         for b in range(blocks):
             nc.tensor.transpose(spread[:, b, :], gate_column[:, b : b + 1].to_broadcast([P, P]), identity[:])
-        shared = stage.tile([P, PAIR * S + 2 * SH], BF16, name="shared", align_bytes=64, offset=0)
-        x_picked = shared[:, SH : SH + PAIR * S]
+        shared = stage.tile([P, 2 * PAIR * S + SH], BF16, name="shared", align_bytes=64, offset=0)
+        gate_picked = shared[:, : PAIR * S].bitcast(F32)
+        x_picked = shared[:, PAIR * S : 2 * PAIR * S]
 
         x_codes = keep.tile([P, S], U32, name="x_codes", align_bytes=64)
         x_scales = keep.tile([P, S], U8, name="x_scales", align_bytes=64)
@@ -104,15 +106,15 @@ def tile_picked_modgate_linnone_lo_kernel(tc, xT, gate, w1, offs, out_0, out_1, 
 
         w_src = w_raw[:].rearrange("p j (m t) -> p m j t", t=PACK)
         MH = P // 2
-        w_early = [shared[:, c0 : c0 + S].rearrange("p (t c) -> p t c", t=PAIR) for c0 in (PAIR * S, 0)]
-        w_late = stage.tile([P, PAIR, P * PACK], BF16, name="w_late", align_bytes=64, offset=7168)
+        w_early = [shared[:, c0 : c0 + S].rearrange("p (t c) -> p t c", t=PAIR) for c0 in (2 * PAIR * S - SH, PAIR * S - SH)]
+        w_late = stage.tile([P, PAIR, P * PACK], BF16, name="w_late", align_bytes=64, offset=11264)
         quantise_x(*halves[1])
         nc.scalar.copy(w_early[0].rearrange("p t (m j) -> p m j t", j=PACK), w_src[:, :MH, :, :PAIR])
         nc.vector.tensor_copy(w_early[1].rearrange("p t (m j) -> p m j t", j=PACK), w_src[:, MH:, :, :PAIR])
         quantise_x(*halves[0])
         nc.scalar.copy(w_late[:].rearrange("p t (m j) -> p m j t", j=PACK), w_src[:, :, :, PAIR:])
 
-        w_codes = keep.tile([P, N], U32, name="w_codes", align_bytes=64)
+        w_codes = keep.tile([P, N], U32, name="w_codes", tag="column_then_codes", align_bytes=64)
         w_scales = keep.tile([P, N], U8, name="w_scales", align_bytes=64)
 
         def quantise_w(c0, c1, grouped_w):
@@ -121,17 +123,16 @@ def tile_picked_modgate_linnone_lo_kernel(tc, xT, gate, w1, offs, out_0, out_1, 
         for t in range(PAIR):
             for h in reversed(range(2)):
                 quantise_w(P * t + MH * h, P * t + MH * (h + 1), w_early[h][:, t, :])
-        gate_picked = stage.tile([P, S], F32, name="gate_picked", align_bytes=64, offset=1024)
-        nc.vector.tensor_copy(gate_picked[:].rearrange("p (n b) -> p n b", b=blocks), spread[:].rearrange("p b n -> p n b"))
+        nc.scalar.copy(gate_picked.rearrange("p (n b) -> p n b", b=blocks), spread[:].rearrange("p b n -> p n b"))
         quantise_w(P * PAIR, N, w_late[:].rearrange("p t c -> p (t c)"))
 
         for t in range(PAIR, PACK):
-            windows.append(stage.tile([P, T], F32, name=f"window{t}", align_bytes=64, offset=4096 * (t - 1)))
+            windows.append(stage.tile([P, T], F32, name=f"window{t}", align_bytes=64, offset=4096 * t))
             nc.gpsimd.memset(windows[t][:], 0.0)
 
         y = [keep.tile([P, S], F32, name=f"y{t}", align_bytes=64) for t in range(PACK)]
         order = [0, 1, 2, 3]
-        pieces = {t: halves[::-1] if t == order[0] else [(0, S)] for t in order}
+        pieces = {t: [halves[1], (0, P), (P, SH)] if t == order[0] else [(0, S)] for t in order}
         for t in order:
             for s0, s1 in pieces[t]:
                 acc = psum.tile([P, s1 - s0], F32, name=f"acc{t}_{s0}")
@@ -144,20 +145,26 @@ def tile_picked_modgate_linnone_lo_kernel(tc, xT, gate, w1, offs, out_0, out_1, 
                     start=True,
                     stop=True,
                 )
-                nc.scalar.copy(y[t][:, s0:s1], acc[:])
+                if (t, s0) == (0, SH):
+                    nc.vector.tensor_copy(y[t][:, s0:s1], acc[:])
+                else:
+                    nc.scalar.copy(y[t][:, s0:s1], acc[:])
 
         out_rows = out_0.rearrange("(p t) c -> p t c", t=PACK)
         grouped = keep.tile([P, T, PACK], BF16, name="out_grouped", align_bytes=64)
         last = PACK - 1
         for t in order:
-            nc.vector.tensor_tensor(windows[t][:].indirect(offsets[:]), y[t][:], gate_picked[:], MULT)
+            nc.vector.tensor_tensor(windows[t][:].indirect(offsets[:]), y[t][:], gate_picked, MULT)
             nc.sync.dma_start(out_rows[:, t, :], windows[t][:])
             if t < last - 1:
                 nc.scalar.copy(grouped[:, :, t], windows[t][:])
             elif t == last - 1:
-                nc.scalar.copy(grouped[:, :HALF, t:], windows[t][:, :HALF].unsqueeze(2).to_broadcast([P, HALF, PAIR]))
+                nc.scalar.copy(
+                    grouped[:, FILL:HALF, t:], windows[t][:, FILL:HALF].unsqueeze(2).to_broadcast([P, HALF - FILL, PAIR])
+                )
                 nc.scalar.copy(grouped[:, HALF:, t], windows[t][:, HALF:])
 
+        nc.vector.tensor_copy(grouped[:, :FILL, last - 1], windows[last - 1][:, :FILL])
         for c0 in range(0, HALF, CHUNK):
             nc.scalar.copy(grouped[:, HALF + c0 : HALF + c0 + CHUNK, last], windows[last][:, HALF + c0 : HALF + c0 + CHUNK])
         for c0 in range(0, HALF, CHUNK):
@@ -178,7 +185,7 @@ def tile_picked_modgate_linnone_lo_kernel(tc, xT, gate, w1, offs, out_0, out_1, 
                 nc.sync.dma_start(words[:, stored:c1], out_codes[:, stored:c1].bitcast(I32))
                 stored = c1
         for q in range(4):
-            queue = nc.sync if q == 0 else nc.scalar
+            queue = nc.sync if q < 2 else nc.scalar
             queue.dma_start(
                 out_2[0, 4 * q : 4 * q + 4, :].bitcast(I32), out_scales[32 * q : 32 * q + 4, :].bitcast(I32)
             )

@@ -35,24 +35,20 @@ def tile_picked_modgate_linnone_lo_kernel(tc, xT, gate, w1, offs, out_0, out_1, 
 
         stage = ctx.enter_context(tc.tile_pool(name="stage", bufs=1))
         gate_row = stage.tile([P, T], F32, name="gate_row", align_bytes=64, offset=0)
-        nc.gpsimd.memset(gate_row[:LAST, :], 0.0)
         offsets = keep.tile([P, S // LIST_ROWS], U16, name="offsets")
         x_rows = xT.rearrange("(p j) c -> p j c", j=PACK)
-        x_raw = {j: keep.tile([P, T], F32, name=f"x_raw{j}", align_bytes=64) for j in range(1, PACK)}
-        x_first = [keep.tile([P, HALF], F32, name=f"x_first{h}", align_bytes=64) for h in range(2)]
-        for h in range(2):
-            nc.sync.dma_start(x_first[h][:], x_rows[:, 0, HALF * h : HALF * (h + 1)])
-        nc.sync.dma_start(offsets[:], offs)
-        nc.sync.dma_start(gate_row[LAST:, :], gate[0:1, :])
-        for j in range(1, PACK):
+        x_raw = [keep.tile([P, T], F32, name=f"x_raw{j}", align_bytes=64) for j in range(PACK)]
+        nc.scalar.dma_start(gate_row[LAST:, :], gate[0:1, :])
+        for j in range(PACK):
             nc.sync.dma_start(x_raw[j][:], x_rows[:, j, :])
+            if j == 0:
+                nc.sync.dma_start(offsets[:], offs)
         w_raw = keep.tile([P, PACK, N], F32, name="w_raw", align_bytes=64)
         nc.sync.dma_start(w_raw[:], w1.rearrange("(p j) c -> p j c", j=PACK))
 
-        warm_in = keep.tile([P, 1], F32, name="warm_in")
-        warm_out = keep.tile([P, 1], F32, name="warm_out")
-        nc.vector.memset(warm_in[:], 0.0)
-        nc.scalar.activation(warm_out[:], warm_in[:], COPY)
+        zero = keep.tile([P, 1], F32, name="zero")
+        nc.vector.memset(zero[:], 0.0)
+        nc.scalar.activation(gate_row[:LAST, :], zero[:LAST, :].to_broadcast([LAST, T]), COPY)
 
         identity = keep.tile([P, P], F32, name="identity")
         make_identity(nc, identity[:])
@@ -71,11 +67,8 @@ def tile_picked_modgate_linnone_lo_kernel(tc, xT, gate, w1, offs, out_0, out_1, 
         woven = x_grouped[:].rearrange("p (s j) -> p s j", j=PACK)
         for j in range(PAIR):
             x_bf = keep.tile([P, T], BF16, name=f"x_bf{j}", align_bytes=64)
-            if j == 1:
-                nc.vector.tensor_copy(x_bf[:], x_raw[j][:])
-            else:
-                for h in range(2):
-                    nc.vector.tensor_copy(x_bf[:, HALF * h : HALF * (h + 1)], x_first[h][:])
+            nc.vector.tensor_copy(x_bf[:], x_raw[j][:])
+            if j == 0:
                 nc.vector.tensor_copy(gate_first[:], gate_row[:].indirect(offsets[:]))
             nc.scalar.activation(woven[:, :, j], x_bf[:].indirect(offsets[:]), COPY)
 
@@ -121,7 +114,7 @@ def tile_picked_modgate_linnone_lo_kernel(tc, xT, gate, w1, offs, out_0, out_1, 
             nc.vector.quantize_mx(out=w_codes[:, c0:c1].bitcast(FP8X4), scales=w_scales[:, c0:c1], in_=grouped_w)
 
         for t in range(PAIR):
-            for h in reversed(range(2)):
+            for h in range(2):
                 quantise_w(P * t + MH * h, P * t + MH * (h + 1), w_early[h][:, t, :])
         nc.scalar.copy(gate_picked.rearrange("p (n b) -> p n b", b=blocks), spread[:].rearrange("p b n -> p n b"))
         quantise_w(P * PAIR, N, w_late[:].rearrange("p t c -> p (t c)"))

@@ -24,6 +24,7 @@ HALF = T // 2
 SH = S // 2
 CHUNK = 256
 FILL = 128
+REST = T // 4
 LAST = P - 1
 
 
@@ -37,18 +38,22 @@ def tile_picked_modgate_linnone_lo_kernel(tc, xT, gate, w1, offs, out_0, out_1, 
         gate_row = stage.tile([P, T], F32, name="gate_row", align_bytes=64, offset=0)
         offsets = keep.tile([P, S // LIST_ROWS], U16, name="offsets")
         x_rows = xT.rearrange("(p j) c -> p j c", j=PACK)
-        x_raw = [keep.tile([P, T], F32, name=f"x_raw{j}", align_bytes=64) for j in range(PACK)]
+        x_raw = {j: keep.tile([P, T], F32, name=f"x_raw{j}", align_bytes=64) for j in range(1, PACK)}
+        first_parts = [(0, T - REST), (T - REST, T)]
+        x_first = [keep.tile([P, c1 - c0], F32, name=f"x_first{c0}", align_bytes=64) for c0, c1 in first_parts]
         nc.scalar.dma_start(gate_row[LAST:, :], gate[0:1, :])
-        for j in range(PACK):
+        for part, (c0, c1) in zip(x_first, first_parts):
+            nc.sync.dma_start(part[:], x_rows[:, 0, c0:c1])
+        nc.sync.dma_start(offsets[:], offs)
+        for j in range(1, PACK):
             nc.sync.dma_start(x_raw[j][:], x_rows[:, j, :])
-            if j == 0:
-                nc.sync.dma_start(offsets[:], offs)
         w_raw = keep.tile([P, PACK, N], F32, name="w_raw", align_bytes=64)
         nc.sync.dma_start(w_raw[:], w1.rearrange("(p j) c -> p j c", j=PACK))
 
         zero = keep.tile([P, 1], F32, name="zero")
         nc.vector.memset(zero[:], 0.0)
-        nc.scalar.activation(gate_row[:LAST, :], zero[:LAST, :].to_broadcast([LAST, T]), COPY)
+        nc.scalar.activation(gate_row[:LAST, :REST], zero[:LAST, :].to_broadcast([LAST, REST]), COPY)
+        nc.gpsimd.memset(gate_row[:LAST, REST:], 0.0)
 
         identity = keep.tile([P, P], F32, name="identity")
         make_identity(nc, identity[:])
@@ -67,8 +72,11 @@ def tile_picked_modgate_linnone_lo_kernel(tc, xT, gate, w1, offs, out_0, out_1, 
         woven = x_grouped[:].rearrange("p (s j) -> p s j", j=PACK)
         for j in range(PAIR):
             x_bf = keep.tile([P, T], BF16, name=f"x_bf{j}", align_bytes=64)
-            nc.vector.tensor_copy(x_bf[:], x_raw[j][:])
-            if j == 0:
+            if j == 1:
+                nc.vector.tensor_copy(x_bf[:], x_raw[j][:])
+            else:
+                for part, (c0, c1) in zip(x_first, first_parts):
+                    nc.vector.tensor_copy(x_bf[:, c0:c1], part[:])
                 nc.vector.tensor_copy(gate_first[:], gate_row[:].indirect(offsets[:]))
             nc.scalar.activation(woven[:, :, j], x_bf[:].indirect(offsets[:]), COPY)
 
@@ -87,10 +95,12 @@ def tile_picked_modgate_linnone_lo_kernel(tc, xT, gate, w1, offs, out_0, out_1, 
         planes = x_picked.rearrange("p (j s) -> p j s", j=PAIR)
         by_entry = x_picked.rearrange("p (j s) -> p s j", j=PAIR)
         nc.vector.tensor_copy(planes[:, 0, :], x_raw[2][:].indirect(offsets[:]))
-        for s0, s1 in reversed(halves):
+        thirds = [halves[1], (0, P), (P, SH)]
+        for s0, s1 in thirds:
             nc.vector.tensor_copy(planes[:, 1, s0:s1], x_raw[3][:].indirect(offs_of(s0, s1)))
         nc.scalar.copy(woven[:, SH:, PAIR:], by_entry[:, SH:, :])
-        nc.vector.tensor_copy(woven[:, :SH, PAIR:], by_entry[:, :SH, :])
+        for s0, s1 in thirds[1:]:
+            nc.vector.tensor_copy(woven[:, s0:s1, PAIR:], by_entry[:, s0:s1, :])
 
         def quantise_x(s0, s1):
             nc.vector.quantize_mx(
@@ -101,10 +111,11 @@ def tile_picked_modgate_linnone_lo_kernel(tc, xT, gate, w1, offs, out_0, out_1, 
         MH = P // 2
         w_early = [shared[:, c0 : c0 + S].rearrange("p (t c) -> p t c", t=PAIR) for c0 in (2 * PAIR * S - SH, PAIR * S - SH)]
         w_late = stage.tile([P, PAIR, P * PACK], BF16, name="w_late", align_bytes=64, offset=11264)
-        quantise_x(*halves[1])
+        quantise_x(*thirds[1])
+        quantise_x(*thirds[0])
         nc.scalar.copy(w_early[0].rearrange("p t (m j) -> p m j t", j=PACK), w_src[:, :MH, :, :PAIR])
         nc.vector.tensor_copy(w_early[1].rearrange("p t (m j) -> p m j t", j=PACK), w_src[:, MH:, :, :PAIR])
-        quantise_x(*halves[0])
+        quantise_x(*thirds[2])
         nc.scalar.copy(w_late[:].rearrange("p t (m j) -> p m j t", j=PACK), w_src[:, :, :, PAIR:])
 
         w_codes = keep.tile([P, N], U32, name="w_codes", tag="column_then_codes", align_bytes=64)

@@ -52,14 +52,14 @@ def tile_picked_modgate_linnone_lo_kernel(tc, xT, gate, w1, offs, out_0, out_1, 
 
         zero = keep.tile([P, 1], F32, name="zero")
         nc.vector.memset(zero[:], 0.0)
-        nc.scalar.activation(gate_row[:LAST, :REST], zero[:LAST, :].to_broadcast([LAST, REST]), COPY)
-        nc.gpsimd.memset(gate_row[:LAST, REST:], 0.0)
+        nc.scalar.activation(gate_row[:LAST, :], zero[:LAST, :].to_broadcast([LAST, T]), COPY)
 
         identity = keep.tile([P, P], F32, name="identity")
         make_identity(nc, identity[:])
-        windows = [keep.tile([P, T], F32, name=f"window{t}", align_bytes=64) for t in range(PAIR)]
-        for t in range(PAIR):
-            nc.vector.memset(windows[t][:], 0.0)
+        windows = [keep.tile([P, T], F32, name=f"window{t}", align_bytes=64) for t in range(PACK)]
+        for t in range(PACK):
+            engine = nc.vector if t < PAIR else nc.gpsimd
+            engine.memset(windows[t][:], 0.0)
 
         halves = [(h * SH, (h + 1) * SH) for h in range(2)]
 
@@ -68,6 +68,8 @@ def tile_picked_modgate_linnone_lo_kernel(tc, xT, gate, w1, offs, out_0, out_1, 
 
         gate_first = keep.tile([P, S], F32, name="gate_first", align_bytes=64)
 
+        blocks = S // P
+        gate_column = keep.tile([P, blocks], F32, name="gate_column", tag="column_then_codes", align_bytes=64)
         x_grouped = keep.tile([P, S * PACK], BF16, name="x_grouped", align_bytes=64)
         woven = x_grouped[:].rearrange("p (s j) -> p s j", j=PACK)
         for j in range(PAIR):
@@ -79,10 +81,9 @@ def tile_picked_modgate_linnone_lo_kernel(tc, xT, gate, w1, offs, out_0, out_1, 
                     nc.vector.tensor_copy(x_bf[:, c0:c1], part[:])
                 nc.vector.tensor_copy(gate_first[:], gate_row[:].indirect(offsets[:]))
             nc.scalar.activation(woven[:, :, j], x_bf[:].indirect(offsets[:]), COPY)
+            if j == 0:
+                nc.gpsimd.dma_start(gate_column[:], gate_first[LAST:, :].rearrange("o (n b) -> o n b", b=blocks))
 
-        blocks = S // P
-        gate_column = keep.tile([P, blocks], F32, name="gate_column", tag="column_then_codes", align_bytes=64)
-        nc.gpsimd.dma_start(gate_column[:], gate_first[LAST:, :].rearrange("o (n b) -> o n b", b=blocks))
         spread = psum.tile([P, blocks, P], F32, name="spread")
         for b in range(blocks):
             nc.tensor.transpose(spread[:, b, :], gate_column[:, b : b + 1].to_broadcast([P, P]), identity[:])
@@ -110,7 +111,7 @@ def tile_picked_modgate_linnone_lo_kernel(tc, xT, gate, w1, offs, out_0, out_1, 
         w_src = w_raw[:].rearrange("p j (m t) -> p m j t", t=PACK)
         MH = P // 2
         w_early = [shared[:, c0 : c0 + S].rearrange("p (t c) -> p t c", t=PAIR) for c0 in (2 * PAIR * S - SH, PAIR * S - SH)]
-        w_late = stage.tile([P, PAIR, P * PACK], BF16, name="w_late", align_bytes=64, offset=11264)
+        w_late = keep.tile([P, PAIR, P * PACK], BF16, name="w_late", align_bytes=64)
         quantise_x(*thirds[1])
         quantise_x(*thirds[0])
         nc.scalar.copy(w_early[0].rearrange("p t (m j) -> p m j t", j=PACK), w_src[:, :MH, :, :PAIR])
@@ -127,16 +128,12 @@ def tile_picked_modgate_linnone_lo_kernel(tc, xT, gate, w1, offs, out_0, out_1, 
         for t in range(PAIR):
             for h in range(2):
                 quantise_w(P * t + MH * h, P * t + MH * (h + 1), w_early[h][:, t, :])
-        nc.scalar.copy(gate_picked.rearrange("p (n b) -> p n b", b=blocks), spread[:].rearrange("p b n -> p n b"))
+        nc.vector.tensor_copy(gate_picked.rearrange("p (n b) -> p n b", b=blocks), spread[:].rearrange("p b n -> p n b"))
         quantise_w(P * PAIR, N, w_late[:].rearrange("p t c -> p (t c)"))
-
-        for t in range(PAIR, PACK):
-            windows.append(stage.tile([P, T], F32, name=f"window{t}", align_bytes=64, offset=4096 * t))
-            nc.gpsimd.memset(windows[t][:], 0.0)
 
         y = [keep.tile([P, S], F32, name=f"y{t}", align_bytes=64) for t in range(PACK)]
         order = [0, 1, 2, 3]
-        pieces = {t: [halves[1], (0, P), (P, SH)] if t == order[0] else [(0, S)] for t in order}
+        pieces = {t: halves[::-1] if t == order[0] else [(0, S)] for t in order}
         for t in order:
             for s0, s1 in pieces[t]:
                 acc = psum.tile([P, s1 - s0], F32, name=f"acc{t}_{s0}")
@@ -149,10 +146,7 @@ def tile_picked_modgate_linnone_lo_kernel(tc, xT, gate, w1, offs, out_0, out_1, 
                     start=True,
                     stop=True,
                 )
-                if (t, s0) == (0, SH):
-                    nc.vector.tensor_copy(y[t][:, s0:s1], acc[:])
-                else:
-                    nc.scalar.copy(y[t][:, s0:s1], acc[:])
+                nc.scalar.copy(y[t][:, s0:s1], acc[:])
 
         out_rows = out_0.rearrange("(p t) c -> p t c", t=PACK)
         grouped = keep.tile([P, T, PACK], BF16, name="out_grouped", align_bytes=64)

@@ -128,12 +128,12 @@ def tile_picked_modgate_linnone_lo_kernel(tc, xT, gate, w1, offs, out_0, out_1, 
         for t in range(PAIR):
             for h in range(2):
                 quantise_w(P * t + MH * h, P * t + MH * (h + 1), w_early[h][:, t, :])
-        nc.vector.tensor_copy(gate_picked.rearrange("p (n b) -> p n b", b=blocks), spread[:].rearrange("p b n -> p n b"))
+        nc.scalar.copy(gate_picked.rearrange("p (n b) -> p n b", b=blocks), spread[:].rearrange("p b n -> p n b"))
         quantise_w(P * PAIR, N, w_late[:].rearrange("p t c -> p (t c)"))
 
         y = [keep.tile([P, S], F32, name=f"y{t}", align_bytes=64) for t in range(PACK)]
         order = [0, 1, 2, 3]
-        pieces = {t: halves[::-1] if t == order[0] else [(0, S)] for t in order}
+        pieces = {t: thirds if t == order[0] else [(0, S)] for t in order}
         for t in order:
             for s0, s1 in pieces[t]:
                 acc = psum.tile([P, s1 - s0], F32, name=f"acc{t}_{s0}")
@@ -146,7 +146,10 @@ def tile_picked_modgate_linnone_lo_kernel(tc, xT, gate, w1, offs, out_0, out_1, 
                     start=True,
                     stop=True,
                 )
-                nc.scalar.copy(y[t][:, s0:s1], acc[:])
+                if (t, s0) == (0, SH):
+                    nc.vector.tensor_copy(y[t][:, s0:s1], acc[:])
+                else:
+                    nc.scalar.copy(y[t][:, s0:s1], acc[:])
 
         out_rows = out_0.rearrange("(p t) c -> p t c", t=PACK)
         grouped = keep.tile([P, T, PACK], BF16, name="out_grouped", align_bytes=64)

@@ -19,12 +19,12 @@ MULT = mybir.AluOpType.mult
 P = 128
 PACK = 4
 PAIR = 2
+LINE = 4
 LIST_ROWS = 16
-HALF = T // 2
 SH = S // 2
+SQ = S // 4
 CHUNK = 256
-FILL = 128
-REST = T // 4
+SPLIT = 576
 LAST = P - 1
 
 
@@ -34,20 +34,16 @@ def tile_picked_modgate_linnone_lo_kernel(tc, xT, gate, w1, offs, out_0, out_1, 
         keep = ctx.enter_context(tc.tile_pool(name="keep", bufs=1))
         psum = ctx.enter_context(tc.psum_pool(name="psum", bufs=1))
 
-        stage = ctx.enter_context(tc.tile_pool(name="stage", bufs=1))
-        gate_row = stage.tile([P, T], F32, name="gate_row", align_bytes=64, offset=0)
+        gate_row = keep.tile([P, T], F32, name="gate_row", align_bytes=64)
         offsets = keep.tile([P, S // LIST_ROWS], U16, name="offsets")
         x_rows = xT.rearrange("(p j) c -> p j c", j=PACK)
-        x_raw = {j: keep.tile([P, T], F32, name=f"x_raw{j}", align_bytes=64) for j in range(1, PACK)}
-        first_parts = [(0, T - REST), (T - REST, T)]
-        x_first = [keep.tile([P, c1 - c0], F32, name=f"x_first{c0}", align_bytes=64) for c0, c1 in first_parts]
+        x_raw = [keep.tile([P, T], F32, name=f"x_raw{j}", align_bytes=64) for j in range(PACK)]
+        w_raw = keep.tile([P, PACK, N], F32, name="w_raw", align_bytes=64)
         nc.scalar.dma_start(gate_row[LAST:, :], gate[0:1, :])
-        for part, (c0, c1) in zip(x_first, first_parts):
-            nc.sync.dma_start(part[:], x_rows[:, 0, c0:c1])
+        nc.sync.dma_start(x_raw[0][:], x_rows[:, 0, :])
         nc.sync.dma_start(offsets[:], offs)
         for j in range(1, PACK):
             nc.sync.dma_start(x_raw[j][:], x_rows[:, j, :])
-        w_raw = keep.tile([P, PACK, N], F32, name="w_raw", align_bytes=64)
         nc.sync.dma_start(w_raw[:], w1.rearrange("(p j) c -> p j c", j=PACK))
 
         zero = keep.tile([P, 1], F32, name="zero")
@@ -61,115 +57,102 @@ def tile_picked_modgate_linnone_lo_kernel(tc, xT, gate, w1, offs, out_0, out_1, 
             engine = nc.vector if t < PAIR else nc.gpsimd
             engine.memset(windows[t][:], 0.0)
 
-        halves = [(h * SH, (h + 1) * SH) for h in range(2)]
-
         def offs_of(s0, s1):
             return offsets[:, s0 // LIST_ROWS : s1 // LIST_ROWS]
 
-        gate_first = keep.tile([P, S], F32, name="gate_first", align_bytes=64)
-
         blocks = S // P
-        gate_column = keep.tile([P, blocks], F32, name="gate_column", tag="column_then_codes", align_bytes=64)
-        x_grouped = keep.tile([P, S * PACK], BF16, name="x_grouped", align_bytes=64)
-        woven = x_grouped[:].rearrange("p (s j) -> p s j", j=PACK)
-        for j in range(PAIR):
-            x_bf = keep.tile([P, T], BF16, name=f"x_bf{j}", align_bytes=64)
-            if j == 1:
-                nc.vector.tensor_copy(x_bf[:], x_raw[j][:])
-            else:
-                for part, (c0, c1) in zip(x_first, first_parts):
-                    nc.vector.tensor_copy(x_bf[:, c0:c1], part[:])
-                nc.vector.tensor_copy(gate_first[:], gate_row[:].indirect(offsets[:]))
-            nc.scalar.activation(woven[:, :, j], x_bf[:].indirect(offsets[:]), COPY)
-            if j == 0:
-                nc.gpsimd.dma_start(gate_column[:], gate_first[LAST:, :].rearrange("o (n b) -> o n b", b=blocks))
-
+        gate_first = keep.tile([P, S], F32, name="gate_first", align_bytes=64)
+        nc.vector.tensor_copy(gate_first[:], gate_row[:].indirect(offsets[:]))
+        turned = psum.tile([P, blocks, P], F32, name="turned")
+        for b in range(blocks):
+            nc.tensor.transpose(turned[:, b, :], gate_first[:, P * b : P * (b + 1)], identity[:])
+        gate_column = keep.tile([P, blocks], F32, name="gate_column")
+        nc.vector.tensor_copy(gate_column[:], turned[:, :, LAST])
         spread = psum.tile([P, blocks, P], F32, name="spread")
         for b in range(blocks):
             nc.tensor.transpose(spread[:, b, :], gate_column[:, b : b + 1].to_broadcast([P, P]), identity[:])
-        shared = stage.tile([P, 2 * PAIR * S + SH], BF16, name="shared", align_bytes=64, offset=0)
-        gate_picked = shared[:, : PAIR * S].bitcast(F32)
-        x_picked = shared[:, PAIR * S : 2 * PAIR * S]
+        gate_picked = keep.tile([P, S], F32, name="gate_picked", align_bytes=64)
+        nc.vector.tensor_copy(gate_picked[:], spread[:].rearrange("p b n -> p (b n)"))
 
+        x_picked = keep.tile([P, PACK, S], BF16, name="x_picked", align_bytes=64)
+        last = PACK - 1
+        for j in range(last):
+            nc.scalar.activation(x_picked[:, j, :], x_raw[j][:].indirect(offsets[:]), COPY)
+        nc.vector.tensor_copy(x_picked[:, last, :SH], x_raw[last][:].indirect(offs_of(0, SH)))
+        nc.scalar.activation(x_picked[:, last, SH:], x_raw[last][:].indirect(offs_of(SH, S)), COPY)
+
+        def weave(copy, dst, src):
+            copy(
+                dst.rearrange("p (c i t) -> p c t i", i=LINE, t=PACK),
+                src.rearrange("p t (c i) -> p c t i", i=LINE),
+            )
+
+        x_grouped = keep.tile([P, S * PACK], BF16, name="x_grouped", align_bytes=64)
         x_codes = keep.tile([P, S], U32, name="x_codes", align_bytes=64)
         x_scales = keep.tile([P, S], U8, name="x_scales", align_bytes=64)
-        planes = x_picked.rearrange("p (j s) -> p j s", j=PAIR)
-        by_entry = x_picked.rearrange("p (j s) -> p s j", j=PAIR)
-        nc.vector.tensor_copy(planes[:, 0, :], x_raw[2][:].indirect(offsets[:]))
-        thirds = [halves[1], (0, P), (P, SH)]
-        for s0, s1 in thirds:
-            nc.vector.tensor_copy(planes[:, 1, s0:s1], x_raw[3][:].indirect(offs_of(s0, s1)))
-        nc.scalar.copy(woven[:, SH:, PAIR:], by_entry[:, SH:, :])
-        for s0, s1 in thirds[1:]:
-            nc.vector.tensor_copy(woven[:, s0:s1, PAIR:], by_entry[:, s0:s1, :])
-
-        def quantise_x(s0, s1):
+        for copy, s0, s1 in (
+            (nc.vector.tensor_copy, 0, SH),
+            (nc.scalar.copy, S - SQ, S),
+            (nc.vector.tensor_copy, SH, S - SQ),
+        ):
+            weave(copy, x_grouped[:, PACK * s0 : PACK * s1], x_picked[:, :, s0:s1])
+        for s0 in (0, SH):
+            s1 = s0 + SH
             nc.vector.quantize_mx(
                 out=x_codes[:, s0:s1].bitcast(FP8X4), scales=x_scales[:, s0:s1], in_=x_grouped[:, PACK * s0 : PACK * s1]
             )
 
         w_src = w_raw[:].rearrange("p j (m t) -> p m j t", t=PACK)
-        MH = P // 2
-        w_early = [shared[:, c0 : c0 + S].rearrange("p (t c) -> p t c", t=PAIR) for c0 in (2 * PAIR * S - SH, PAIR * S - SH)]
-        w_late = keep.tile([P, PAIR, P * PACK], BF16, name="w_late", align_bytes=64)
-        quantise_x(*thirds[1])
-        quantise_x(*thirds[0])
-        nc.scalar.copy(w_early[0].rearrange("p t (m j) -> p m j t", j=PACK), w_src[:, :MH, :, :PAIR])
-        nc.vector.tensor_copy(w_early[1].rearrange("p t (m j) -> p m j t", j=PACK), w_src[:, MH:, :, :PAIR])
-        quantise_x(*thirds[2])
-        nc.scalar.copy(w_late[:].rearrange("p t (m j) -> p m j t", j=PACK), w_src[:, :, :, PAIR:])
-
-        w_codes = keep.tile([P, N], U32, name="w_codes", tag="column_then_codes", align_bytes=64)
+        w_codes = keep.tile([P, N], U32, name="w_codes", align_bytes=64)
         w_scales = keep.tile([P, N], U8, name="w_scales", align_bytes=64)
+        w_dealt = [keep.tile([P, PAIR, P * PACK], BF16, name=f"w_dealt{h}", align_bytes=64) for h in range(2)]
+        for h, copy in enumerate((nc.vector.tensor_copy, nc.scalar.copy)):
+            copy(w_dealt[h][:].rearrange("p t (m j) -> p m j t", j=PACK), w_src[:, :, :, PAIR * h : PAIR * (h + 1)])
 
         def quantise_w(c0, c1, grouped_w):
             nc.vector.quantize_mx(out=w_codes[:, c0:c1].bitcast(FP8X4), scales=w_scales[:, c0:c1], in_=grouped_w)
 
         for t in range(PAIR):
-            for h in range(2):
-                quantise_w(P * t + MH * h, P * t + MH * (h + 1), w_early[h][:, t, :])
-        nc.scalar.copy(gate_picked.rearrange("p (n b) -> p n b", b=blocks), spread[:].rearrange("p b n -> p n b"))
-        quantise_w(P * PAIR, N, w_late[:].rearrange("p t c -> p (t c)"))
+            quantise_w(P * t, P * (t + 1), w_dealt[0][:, t, :])
+        quantise_w(P * PAIR, N, w_dealt[1][:].rearrange("p t c -> p (t c)"))
 
         y = [keep.tile([P, S], F32, name=f"y{t}", align_bytes=64) for t in range(PACK)]
-        order = [0, 1, 2, 3]
-        pieces = {t: thirds if t == order[0] else [(0, S)] for t in order}
-        for t in order:
-            for s0, s1 in pieces[t]:
-                acc = psum.tile([P, s1 - s0], F32, name=f"acc{t}_{s0}")
-                nc.tensor.matmul_mx(
-                    out=acc[:],
-                    lhsT=w_codes[:, P * t : P * (t + 1)].bitcast(FP8X4),
-                    lhsT_scale=w_scales[:, P * t : P * (t + 1)],
-                    rhs=x_codes[:, s0:s1].bitcast(FP8X4),
-                    rhs_scale=x_scales[:, s0:s1],
-                    start=True,
-                    stop=True,
-                )
-                if (t, s0) == (0, SH):
-                    nc.vector.tensor_copy(y[t][:, s0:s1], acc[:])
-                else:
-                    nc.scalar.copy(y[t][:, s0:s1], acc[:])
+        for t in range(PACK):
+            acc = psum.tile([P, S], F32, name=f"acc{t}")
+            nc.tensor.matmul_mx(
+                out=acc[:],
+                lhsT=w_codes[:, P * t : P * (t + 1)].bitcast(FP8X4),
+                lhsT_scale=w_scales[:, P * t : P * (t + 1)],
+                rhs=x_codes[:].bitcast(FP8X4),
+                rhs_scale=x_scales[:],
+                start=True,
+                stop=True,
+            )
+            if t % 2 == 0:
+                nc.scalar.copy(y[t][:], acc[:])
+            else:
+                nc.vector.tensor_tensor(y[t][:], acc[:], gate_picked[:], MULT)
 
         out_rows = out_0.rearrange("(p t) c -> p t c", t=PACK)
-        grouped = keep.tile([P, T, PACK], BF16, name="out_grouped", align_bytes=64)
-        last = PACK - 1
-        for t in order:
-            nc.vector.tensor_tensor(windows[t][:].indirect(offsets[:]), y[t][:], gate_picked, MULT)
+        shares = [(0, SPLIT, nc.vector.tensor_copy), (SPLIT, T, nc.scalar.copy)]
+        staged = [keep.tile([P, PACK, c1 - c0], F32, name=f"staged{c0}", align_bytes=64) for c0, c1, copy in shares]
+        for t in range(PACK):
+            if t % 2 == 0:
+                nc.vector.tensor_tensor(windows[t][:].indirect(offsets[:]), y[t][:], gate_picked[:], MULT)
+            else:
+                for s0 in (0, SH):
+                    nc.scalar.activation(windows[t][:].indirect(offs_of(s0, s0 + SH)), y[t][:, s0 : s0 + SH], COPY)
+            if t < PAIR:
+                for tile, (c0, c1, copy) in zip(staged, shares):
+                    nc.sync.dma_start(tile[:, t, :], windows[t][:, c0:c1])
             nc.sync.dma_start(out_rows[:, t, :], windows[t][:])
-            if t < last - 1:
-                nc.scalar.copy(grouped[:, :, t], windows[t][:])
-            elif t == last - 1:
-                nc.scalar.copy(
-                    grouped[:, FILL:HALF, t:], windows[t][:, FILL:HALF].unsqueeze(2).to_broadcast([P, HALF - FILL, PAIR])
-                )
-                nc.scalar.copy(grouped[:, HALF:, t], windows[t][:, HALF:])
 
-        nc.vector.tensor_copy(grouped[:, :FILL, last - 1], windows[last - 1][:, :FILL])
-        for c0 in range(0, HALF, CHUNK):
-            nc.scalar.copy(grouped[:, HALF + c0 : HALF + c0 + CHUNK, last], windows[last][:, HALF + c0 : HALF + c0 + CHUNK])
-        for c0 in range(0, HALF, CHUNK):
-            nc.vector.tensor_copy(grouped[:, c0 : c0 + CHUNK, last], windows[last][:, c0 : c0 + CHUNK])
+        grouped = keep.tile([P, T * PACK], BF16, name="out_grouped", align_bytes=64)
+        for tile, (c0, c1, copy), order in zip(staged, shares, ((3, 2), (2, 3))):
+            for t in order:
+                copy(tile[:, t, :], windows[t][:, c0:c1])
+            for a0, a1 in ((c0, c0 + CHUNK), (c0 + CHUNK, c1)):
+                weave(copy, grouped[:, PACK * a0 : PACK * a1], tile[:, :, a0 - c0 : a1 - c0])
 
         out_codes = keep.tile([P, T], U32, name="out_codes", align_bytes=64)
         out_scales = keep.tile([P, T], U8, name="out_scales", align_bytes=64)
@@ -178,11 +161,9 @@ def tile_picked_modgate_linnone_lo_kernel(tc, xT, gate, w1, offs, out_0, out_1, 
         for c0 in range(0, T, CHUNK):
             c1 = c0 + CHUNK
             nc.vector.quantize_mx(
-                out=out_codes[:, c0:c1].bitcast(FP8X4),
-                scales=out_scales[:, c0:c1],
-                in_=grouped[:, c0:c1, :].rearrange("p c t -> p (c t)"),
+                out=out_codes[:, c0:c1].bitcast(FP8X4), scales=out_scales[:, c0:c1], in_=grouped[:, PACK * c0 : PACK * c1]
             )
-            if c1 >= HALF:
+            if c1 >= 2 * CHUNK:
                 nc.sync.dma_start(words[:, stored:c1], out_codes[:, stored:c1].bitcast(I32))
                 stored = c1
         for q in range(4):

@@ -15,6 +15,7 @@ U8 = mybir.dt.uint8
 FP8X4 = mybir.dt.float8_e4m3fn_x4
 COPY = mybir.ActivationFunctionType.Copy
 MULT = mybir.AluOpType.mult
+ADD = mybir.AluOpType.add
 
 P = 128
 PACK = 4
@@ -24,7 +25,7 @@ LIST_ROWS = 16
 SH = S // 2
 SQ = S // 4
 CHUNK = 256
-SPLIT = 576
+GIVEN = 192
 LAST = P - 1
 
 
@@ -61,8 +62,9 @@ def tile_picked_modgate_linnone_lo_kernel(tc, xT, gate, w1, offs, out_0, out_1, 
             return offsets[:, s0 // LIST_ROWS : s1 // LIST_ROWS]
 
         blocks = S // P
-        gate_first = keep.tile([P, S], F32, name="gate_first", align_bytes=64)
-        nc.vector.tensor_copy(gate_first[:], gate_row[:].indirect(offsets[:]))
+        x_picked = keep.tile([P, PACK, S], BF16, name="x_picked", align_bytes=64)
+        gate_first = x_picked[:, PAIR:, :].rearrange("p j s -> p (j s)").bitcast(F32)
+        nc.vector.tensor_copy(gate_first, gate_row[:].indirect(offsets[:]))
         turned = psum.tile([P, blocks, P], F32, name="turned")
         for b in range(blocks):
             nc.tensor.transpose(turned[:, b, :], gate_first[:, P * b : P * (b + 1)], identity[:])
@@ -71,15 +73,23 @@ def tile_picked_modgate_linnone_lo_kernel(tc, xT, gate, w1, offs, out_0, out_1, 
         spread = psum.tile([P, blocks, P], F32, name="spread")
         for b in range(blocks):
             nc.tensor.transpose(spread[:, b, :], gate_column[:, b : b + 1].to_broadcast([P, P]), identity[:])
-        gate_picked = keep.tile([P, S], F32, name="gate_picked", align_bytes=64)
-        nc.vector.tensor_copy(gate_picked[:], spread[:].rearrange("p b n -> p (b n)"))
 
-        x_picked = keep.tile([P, PACK, S], BF16, name="x_picked", align_bytes=64)
         last = PACK - 1
-        for j in range(last):
-            nc.scalar.activation(x_picked[:, j, :], x_raw[j][:].indirect(offsets[:]), COPY)
-        nc.vector.tensor_copy(x_picked[:, last, :SH], x_raw[last][:].indirect(offs_of(0, SH)))
-        nc.scalar.activation(x_picked[:, last, SH:], x_raw[last][:].indirect(offs_of(SH, S)), COPY)
+
+        def gather(on_vector, j, s0, s1):
+            picked = x_raw[j][:].indirect(offs_of(s0, s1))
+            if on_vector:
+                nc.vector.tensor_copy(x_picked[:, j, s0:s1], picked)
+            else:
+                nc.scalar.activation(x_picked[:, j, s0:s1], picked, COPY)
+
+        for j in range(PAIR):
+            gather(False, j, 0, S)
+        gather(True, PAIR, 0, SH)
+        gather(False, PAIR, SH, S)
+        gather(True, last, 0, SQ)
+        for s0 in range(SQ, S, SQ):
+            gather(False, last, s0, s0 + SQ)
 
         def weave(copy, dst, src):
             copy(
@@ -90,69 +100,102 @@ def tile_picked_modgate_linnone_lo_kernel(tc, xT, gate, w1, offs, out_0, out_1, 
         x_grouped = keep.tile([P, S * PACK], BF16, name="x_grouped", align_bytes=64)
         x_codes = keep.tile([P, S], U32, name="x_codes", align_bytes=64)
         x_scales = keep.tile([P, S], U8, name="x_scales", align_bytes=64)
-        for copy, s0, s1 in (
-            (nc.vector.tensor_copy, 0, SH),
-            (nc.scalar.copy, S - SQ, S),
-            (nc.vector.tensor_copy, SH, S - SQ),
-        ):
-            weave(copy, x_grouped[:, PACK * s0 : PACK * s1], x_picked[:, :, s0:s1])
-        for s0 in (0, SH):
-            s1 = s0 + SH
+        for q in (1, 0, 2, 3):
+            copy = nc.scalar.copy if q == 3 else nc.vector.tensor_copy
+            weave(copy, x_grouped[:, PACK * SQ * q : PACK * SQ * (q + 1)], x_picked[:, :, SQ * q : SQ * (q + 1)])
+        for s0, s1 in ((0, SH), (SH, S - SQ), (S - SQ, S)):
             nc.vector.quantize_mx(
                 out=x_codes[:, s0:s1].bitcast(FP8X4), scales=x_scales[:, s0:s1], in_=x_grouped[:, PACK * s0 : PACK * s1]
             )
 
-        w_src = w_raw[:].rearrange("p j (m t) -> p m j t", t=PACK)
-        w_codes = keep.tile([P, N], U32, name="w_codes", align_bytes=64)
-        w_scales = keep.tile([P, N], U8, name="w_scales", align_bytes=64)
-        w_dealt = [keep.tile([P, PAIR, P * PACK], BF16, name=f"w_dealt{h}", align_bytes=64) for h in range(2)]
-        for h, copy in enumerate((nc.vector.tensor_copy, nc.scalar.copy)):
-            copy(w_dealt[h][:].rearrange("p t (m j) -> p m j t", j=PACK), w_src[:, :, :, PAIR * h : PAIR * (h + 1)])
+        gate_picked = keep.tile([P, S], F32, name="gate_picked", align_bytes=64)
+        nc.scalar.copy(gate_picked[:], spread[:].rearrange("p b n -> p (b n)"))
 
-        def quantise_w(c0, c1, grouped_w):
-            nc.vector.quantize_mx(out=w_codes[:, c0:c1].bitcast(FP8X4), scales=w_scales[:, c0:c1], in_=grouped_w)
+        w_src = w_raw[:].rearrange("p j (m t) -> p m j t", t=PACK)
+        w_codes = [keep.tile([P, PAIR * P], U32, name=f"w_codes{h}", align_bytes=64) for h in range(2)]
+        w_scales = [keep.tile([P, PAIR * P], U8, name=f"w_scales{h}", align_bytes=64) for h in range(2)]
+        w_dealt = [x_picked[:, PAIR * h : PAIR * (h + 1), :] for h in range(2)]
+        for h, copy in enumerate((nc.vector.tensor_copy, nc.scalar.copy)):
+            copy(w_dealt[h].rearrange("p t (m j) -> p m j t", j=PACK), w_src[:, :, :, PAIR * h : PAIR * (h + 1)])
+
+        def quantise_w(h, c0, c1, grouped_w):
+            nc.vector.quantize_mx(out=w_codes[h][:, c0:c1].bitcast(FP8X4), scales=w_scales[h][:, c0:c1], in_=grouped_w)
 
         for t in range(PAIR):
-            quantise_w(P * t, P * (t + 1), w_dealt[0][:, t, :])
-        quantise_w(P * PAIR, N, w_dealt[1][:].rearrange("p t c -> p (t c)"))
+            quantise_w(0, P * t, P * (t + 1), w_dealt[0][:, t, :])
+        quantise_w(1, 0, P * PAIR, w_dealt[1].rearrange("p t c -> p (t c)"))
 
-        y = [keep.tile([P, S], F32, name=f"y{t}", align_bytes=64) for t in range(PACK)]
-        for t in range(PACK):
-            acc = psum.tile([P, S], F32, name=f"acc{t}")
+        def product(acc, t, s0, s1):
+            h, m0 = t // PAIR, P * (t % PAIR)
             nc.tensor.matmul_mx(
-                out=acc[:],
-                lhsT=w_codes[:, P * t : P * (t + 1)].bitcast(FP8X4),
-                lhsT_scale=w_scales[:, P * t : P * (t + 1)],
-                rhs=x_codes[:].bitcast(FP8X4),
-                rhs_scale=x_scales[:],
+                out=acc,
+                lhsT=w_codes[h][:, m0 : m0 + P].bitcast(FP8X4),
+                lhsT_scale=w_scales[h][:, m0 : m0 + P],
+                rhs=x_codes[:, s0:s1].bitcast(FP8X4),
+                rhs_scale=x_scales[:, s0:s1],
                 start=True,
                 stop=True,
             )
-            if t % 2 == 0:
-                nc.scalar.copy(y[t][:], acc[:])
+
+        paired = keep.tile([P, PAIR * T], F32, name="paired", align_bytes=64)
+        y = [
+            paired[:, T + SQ : T + SQ + S] if t == PAIR else keep.tile([P, S], F32, name=f"y{t}", align_bytes=64)[:]
+            for t in range(PACK)
+        ]
+        pieces = ((0, 0, SQ), (0, SQ, S), (2, 0, S), (1, 0, S), (3, 0, S))
+        banks = {}
+        for t, s0, s1 in pieces:
+            banks[t, s0] = psum.tile([P, S], F32, name=f"acc{t}_{s0}")[:, : s1 - s0]
+            cuts = (SQ, SH, S) if s0 == SQ else (s0, s1)
+            for a0, a1 in zip(cuts, cuts[1:]):
+                product(banks[t, s0][:, a0 - s0 : a1 - s0], t, a0, a1)
+
+        def weigh(t, s0, s1):
+            nc.vector.tensor_tensor(y[t][:, s0:s1], banks[t, s0], gate_picked[:, s0:s1], MULT)
+
+        def scatter(on_vector, t, s0, s1):
+            window = windows[t][:].indirect(offs_of(s0, s1))
+            if on_vector:
+                nc.vector.tensor_copy(window, y[t][:, s0:s1])
             else:
-                nc.vector.tensor_tensor(y[t][:], acc[:], gate_picked[:], MULT)
+                nc.scalar.activation(window, y[t][:, s0:s1], COPY)
 
         out_rows = out_0.rearrange("(p t) c -> p t c", t=PACK)
-        shares = [(0, SPLIT, nc.vector.tensor_copy), (SPLIT, T, nc.scalar.copy)]
-        staged = [keep.tile([P, PACK, c1 - c0], F32, name=f"staged{c0}", align_bytes=64) for c0, c1, copy in shares]
-        for t in range(PACK):
-            if t % 2 == 0:
-                nc.vector.tensor_tensor(windows[t][:].indirect(offsets[:]), y[t][:], gate_picked[:], MULT)
-            else:
-                for s0 in (0, SH):
-                    nc.scalar.activation(windows[t][:].indirect(offs_of(s0, s0 + SH)), y[t][:, s0 : s0 + SH], COPY)
-            if t < PAIR:
-                for tile, (c0, c1, copy) in zip(staged, shares):
-                    nc.sync.dma_start(tile[:, t, :], windows[t][:, c0:c1])
+        pairs = paired[:].bitcast(BF16).rearrange("p (u c e) -> p u c e", u=PAIR, e=PAIR)
+        pair_words = paired[:].bitcast(U32).rearrange("p (u c) -> p u c", u=PAIR)
+
+        def finish_early(t):
+            nc.sync.dma_start(out_rows[:, t, :], windows[t][:])
+            nc.gpsimd.tensor_scalar(pairs[:, 0, :, t], windows[t][:], 1.0, -0.0, MULT, ADD)
+
+        for piece in pieces:
+            weigh(*piece)
+        scatter(False, 0, 0, SQ)
+        scatter(False, 0, SQ, S)
+        finish_early(0)
+        scatter(True, 1, 0, S)
+        finish_early(1)
+        scatter(False, 2, 0, GIVEN)
+        scatter(True, 2, GIVEN, S)
+        scatter(False, 3, 0, SH)
+        scatter(False, 3, SH, S)
+        for t in (2, 3):
             nc.sync.dma_start(out_rows[:, t, :], windows[t][:])
 
+        def stage(t, c0, c1):
+            nc.vector.tensor_copy(pairs[:, 1, c0:c1, t % PAIR], windows[t][:, c0:c1])
+
         grouped = keep.tile([P, T * PACK], BF16, name="out_grouped", align_bytes=64)
-        for tile, (c0, c1, copy), order in zip(staged, shares, ((3, 2), (2, 3))):
-            for t in order:
-                copy(tile[:, t, :], windows[t][:, c0:c1])
-            for a0, a1 in ((c0, c0 + CHUNK), (c0 + CHUNK, c1)):
-                weave(copy, grouped[:, PACK * a0 : PACK * a1], tile[:, :, a0 - c0 : a1 - c0])
+        stage(PAIR, 0, T)
+        for c0, c1 in ((0, CHUNK), (2 * CHUNK, T), (CHUNK, 2 * CHUNK)):
+            stage(last, c0, c1)
+        for c0 in range(0, T, CHUNK):
+            dst = grouped[:, PACK * c0 : PACK * (c0 + CHUNK)].bitcast(U32).rearrange("p (c i u) -> p c u i", i=LINE, u=PAIR)
+            src = pair_words[:, :, c0 : c0 + CHUNK].rearrange("p u (c i) -> p c u i", i=LINE)
+            if c0 == CHUNK:
+                nc.vector.tensor_copy(dst.bitcast(I32), src.bitcast(I32))
+            else:
+                nc.scalar.copy(dst, src)
 
         out_codes = keep.tile([P, T], U32, name="out_codes", align_bytes=64)
         out_scales = keep.tile([P, T], U8, name="out_scales", align_bytes=64)

@@ -25,7 +25,7 @@ LIST_ROWS = 16
 SH = S // 2
 SQ = S // 4
 CHUNK = 256
-GIVEN = 192
+GIVEN = 160
 LAST = P - 1
 
 
@@ -41,32 +41,35 @@ def tile_picked_modgate_linnone_lo_kernel(tc, xT, gate, w1, offs, out_0, out_1, 
         x_raw = [keep.tile([P, T], F32, name=f"x_raw{j}", align_bytes=64) for j in range(PACK)]
         w_raw = keep.tile([P, PACK, N], F32, name="w_raw", align_bytes=64)
         nc.scalar.dma_start(gate_row[LAST:, :], gate[0:1, :])
-        nc.sync.dma_start(x_raw[0][:], x_rows[:, 0, :])
+        nc.sync.dma_start(x_raw[0][:, :CHUNK], x_rows[:, 0, :CHUNK])
         nc.sync.dma_start(offsets[:], offs)
+        nc.sync.dma_start(x_raw[0][:, CHUNK:], x_rows[:, 0, CHUNK:])
         for j in range(1, PACK):
             nc.sync.dma_start(x_raw[j][:], x_rows[:, j, :])
         nc.sync.dma_start(w_raw[:], w1.rearrange("(p j) c -> p j c", j=PACK))
 
         zero = keep.tile([P, 1], F32, name="zero")
         nc.vector.memset(zero[:], 0.0)
-        nc.scalar.activation(gate_row[:LAST, :], zero[:LAST, :].to_broadcast([LAST, T]), COPY)
+        nc.scalar.activation(gate_row[:LAST, :CHUNK], zero[:LAST, :].to_broadcast([LAST, CHUNK]), COPY)
+        nc.vector.memset(gate_row[:LAST, CHUNK:], 0.0)
 
         identity = keep.tile([P, P], F32, name="identity")
         make_identity(nc, identity[:])
         windows = [keep.tile([P, T], F32, name=f"window{t}", align_bytes=64) for t in range(PACK)]
         for t in range(PACK):
-            engine = nc.vector if t < PAIR else nc.gpsimd
+            engine = nc.vector if t == 0 else nc.gpsimd
             engine.memset(windows[t][:], 0.0)
 
         def offs_of(s0, s1):
             return offsets[:, s0 // LIST_ROWS : s1 // LIST_ROWS]
 
         blocks = S // P
-        x_picked = keep.tile([P, PACK, S], BF16, name="x_picked", align_bytes=64)
-        gate_first = x_picked[:, PAIR:, :].rearrange("p j s -> p (j s)").bitcast(F32)
+        room = keep.tile([P, PACK * S + SQ], BF16, name="room", align_bytes=64)
+        x_picked = room[:, : PACK * S].rearrange("p (j s) -> p j s", j=PACK)
+        gate_first = room[:, PAIR * S + SQ :].bitcast(F32)
         nc.vector.tensor_copy(gate_first, gate_row[:].indirect(offsets[:]))
         turned = psum.tile([P, blocks, P], F32, name="turned")
-        for b in range(blocks):
+        for b in (0, 2, 3, 1):
             nc.tensor.transpose(turned[:, b, :], gate_first[:, P * b : P * (b + 1)], identity[:])
         gate_column = keep.tile([P, blocks], F32, name="gate_column")
         nc.vector.tensor_copy(gate_column[:], turned[:, :, LAST])
@@ -85,8 +88,8 @@ def tile_picked_modgate_linnone_lo_kernel(tc, xT, gate, w1, offs, out_0, out_1, 
 
         for j in range(PAIR):
             gather(False, j, 0, S)
-        gather(True, PAIR, 0, SH)
-        gather(False, PAIR, SH, S)
+        gather(False, PAIR, 0, SH)
+        gather(True, PAIR, SH, S)
         gather(True, last, 0, SQ)
         for s0 in range(SQ, S, SQ):
             gather(False, last, s0, s0 + SQ)
@@ -139,7 +142,7 @@ def tile_picked_modgate_linnone_lo_kernel(tc, xT, gate, w1, offs, out_0, out_1, 
 
         paired = keep.tile([P, PAIR * T], F32, name="paired", align_bytes=64)
         y = [
-            paired[:, T + SQ : T + SQ + S] if t == PAIR else keep.tile([P, S], F32, name=f"y{t}", align_bytes=64)[:]
+            keep.tile([P, S], F32, name=f"y{t}", align_bytes=64)[:] if t < PAIR else paired[:, t * S : (t + 1) * S]
             for t in range(PACK)
         ]
         pieces = ((0, 0, SQ), (0, SQ, S), (2, 0, S), (1, 0, S), (3, 0, S))
@@ -182,33 +185,38 @@ def tile_picked_modgate_linnone_lo_kernel(tc, xT, gate, w1, offs, out_0, out_1, 
         for t in (2, 3):
             nc.sync.dma_start(out_rows[:, t, :], windows[t][:])
 
-        def stage(t, c0, c1):
-            nc.vector.tensor_copy(pairs[:, 1, c0:c1, t % PAIR], windows[t][:, c0:c1])
+        def stage(copy, t, c0, c1):
+            copy(pairs[:, 1, c0:c1, t % PAIR], windows[t][:, c0:c1])
 
         grouped = keep.tile([P, T * PACK], BF16, name="out_grouped", align_bytes=64)
-        stage(PAIR, 0, T)
-        for c0, c1 in ((0, CHUNK), (2 * CHUNK, T), (CHUNK, 2 * CHUNK)):
-            stage(last, c0, c1)
-        for c0 in range(0, T, CHUNK):
+
+        def weave_words(on_vector, c0):
             dst = grouped[:, PACK * c0 : PACK * (c0 + CHUNK)].bitcast(U32).rearrange("p (c i u) -> p c u i", i=LINE, u=PAIR)
             src = pair_words[:, :, c0 : c0 + CHUNK].rearrange("p u (c i) -> p c u i", i=LINE)
-            if c0 == CHUNK:
+            if on_vector:
                 nc.vector.tensor_copy(dst.bitcast(I32), src.bitcast(I32))
             else:
                 nc.scalar.copy(dst, src)
 
+        stage(nc.vector.tensor_copy, PAIR, 0, T - CHUNK)
+        for t in (PAIR, last):
+            stage(nc.scalar.copy, t, T - CHUNK, T)
+        for c0, c1 in ((0, 2 * CHUNK), (2 * CHUNK, T - CHUNK)):
+            stage(nc.vector.tensor_copy, last, c0, c1)
+        for c0 in (0, CHUNK, 3 * CHUNK, 2 * CHUNK):
+            weave_words(c0 < 2 * CHUNK, c0)
+
         out_codes = keep.tile([P, T], U32, name="out_codes", align_bytes=64)
         out_scales = keep.tile([P, T], U8, name="out_scales", align_bytes=64)
         words = out_1[0].rearrange("p c r -> p (c r)").bitcast(I32)
-        stored = 0
-        for c0 in range(0, T, CHUNK):
+        for c0 in (0, CHUNK, 3 * CHUNK, 2 * CHUNK):
             c1 = c0 + CHUNK
             nc.vector.quantize_mx(
                 out=out_codes[:, c0:c1].bitcast(FP8X4), scales=out_scales[:, c0:c1], in_=grouped[:, PACK * c0 : PACK * c1]
             )
-            if c1 >= 2 * CHUNK:
-                nc.sync.dma_start(words[:, stored:c1], out_codes[:, stored:c1].bitcast(I32))
-                stored = c1
+            if c0 > 0:
+                first = 0 if c0 == CHUNK else c0
+                nc.sync.dma_start(words[:, first:c1], out_codes[:, first:c1].bitcast(I32))
         for q in range(4):
             queue = nc.sync if q < 2 else nc.scalar
             queue.dma_start(

@@ -67,9 +67,10 @@ def tile_picked_modgate_linnone_lo_kernel(tc, xT, gate, w1, offs, out_0, out_1, 
         room = keep.tile([P, PACK * S + SQ], BF16, name="room", align_bytes=64)
         x_picked = room[:, : PACK * S].rearrange("p (j s) -> p j s", j=PACK)
         gate_first = room[:, PAIR * S + SQ :].bitcast(F32)
-        nc.vector.tensor_copy(gate_first, gate_row[:].indirect(offsets[:]))
+        for s0 in (SH, 0):
+            nc.vector.tensor_copy(gate_first[:, s0 : s0 + SH], gate_row[:].indirect(offs_of(s0, s0 + SH)))
         turned = psum.tile([P, blocks, P], F32, name="turned")
-        for b in (0, 2, 3, 1):
+        for b in (2, 3, 0, 1):
             nc.tensor.transpose(turned[:, b, :], gate_first[:, P * b : P * (b + 1)], identity[:])
         gate_column = keep.tile([P, blocks], F32, name="gate_column")
         nc.vector.tensor_copy(gate_column[:], turned[:, :, LAST])
@@ -88,8 +89,8 @@ def tile_picked_modgate_linnone_lo_kernel(tc, xT, gate, w1, offs, out_0, out_1, 
 
         for j in range(PAIR):
             gather(False, j, 0, S)
-        gather(False, PAIR, 0, SH)
-        gather(True, PAIR, SH, S)
+        gather(False, PAIR, 0, SQ)
+        gather(True, PAIR, SQ, S)
         gather(True, last, 0, SQ)
         for s0 in range(SQ, S, SQ):
             gather(False, last, s0, s0 + SQ)
@@ -106,10 +107,14 @@ def tile_picked_modgate_linnone_lo_kernel(tc, xT, gate, w1, offs, out_0, out_1, 
         for q in (1, 0, 2, 3):
             copy = nc.scalar.copy if q == 3 else nc.vector.tensor_copy
             weave(copy, x_grouped[:, PACK * SQ * q : PACK * SQ * (q + 1)], x_picked[:, :, SQ * q : SQ * (q + 1)])
-        for s0, s1 in ((0, SH), (SH, S - SQ), (S - SQ, S)):
+
+        def quantise_x(s0, s1):
             nc.vector.quantize_mx(
                 out=x_codes[:, s0:s1].bitcast(FP8X4), scales=x_scales[:, s0:s1], in_=x_grouped[:, PACK * s0 : PACK * s1]
             )
+
+        quantise_x(0, SH)
+        quantise_x(SH, S - SQ)
 
         gate_picked = keep.tile([P, S], F32, name="gate_picked", align_bytes=64)
         nc.scalar.copy(gate_picked[:], spread[:].rearrange("p b n -> p (b n)"))
@@ -120,6 +125,7 @@ def tile_picked_modgate_linnone_lo_kernel(tc, xT, gate, w1, offs, out_0, out_1, 
         w_dealt = [x_picked[:, PAIR * h : PAIR * (h + 1), :] for h in range(2)]
         for h, copy in enumerate((nc.vector.tensor_copy, nc.scalar.copy)):
             copy(w_dealt[h].rearrange("p t (m j) -> p m j t", j=PACK), w_src[:, :, :, PAIR * h : PAIR * (h + 1)])
+        quantise_x(S - SQ, S)
 
         def quantise_w(h, c0, c1, grouped_w):
             nc.vector.quantize_mx(out=w_codes[h][:, c0:c1].bitcast(FP8X4), scales=w_scales[h][:, c0:c1], in_=grouped_w)
@@ -140,12 +146,11 @@ def tile_picked_modgate_linnone_lo_kernel(tc, xT, gate, w1, offs, out_0, out_1, 
                 stop=True,
             )
 
-        paired = keep.tile([P, PAIR * T], F32, name="paired", align_bytes=64)
-        y = [
-            keep.tile([P, S], F32, name=f"y{t}", align_bytes=64)[:] if t < PAIR else paired[:, t * S : (t + 1) * S]
-            for t in range(PACK)
-        ]
-        pieces = ((0, 0, SQ), (0, SQ, S), (2, 0, S), (1, 0, S), (3, 0, S))
+        room_out = keep.tile([P, PAIR * T + SQ], F32, name="room_out", align_bytes=64)
+        paired = room_out[:, : PAIR * T]
+        y = [keep.tile([P, S], F32, name=f"y{t}", align_bytes=64)[:] for t in range(PAIR)]
+        y.extend(room_out[:, c0 : c0 + S] for c0 in (T + SQ, T + SQ + S))
+        pieces = ((0, 0, SQ), (0, SQ, S), (1, 0, S), (2, 0, S), (3, 0, S))
         banks = {}
         for t, s0, s1 in pieces:
             banks[t, s0] = psum.tile([P, S], F32, name=f"acc{t}_{s0}")[:, : s1 - s0]
@@ -164,8 +169,8 @@ def tile_picked_modgate_linnone_lo_kernel(tc, xT, gate, w1, offs, out_0, out_1, 
                 nc.scalar.activation(window, y[t][:, s0:s1], COPY)
 
         out_rows = out_0.rearrange("(p t) c -> p t c", t=PACK)
-        pairs = paired[:].bitcast(BF16).rearrange("p (u c e) -> p u c e", u=PAIR, e=PAIR)
-        pair_words = paired[:].bitcast(U32).rearrange("p (u c) -> p u c", u=PAIR)
+        pairs = paired.bitcast(BF16).rearrange("p (u c e) -> p u c e", u=PAIR, e=PAIR)
+        pair_words = paired.bitcast(U32).rearrange("p (u c) -> p u c", u=PAIR)
 
         def finish_early(t):
             nc.sync.dma_start(out_rows[:, t, :], windows[t][:])

@@ -208,13 +208,13 @@ def tile_picked_modgate_linnone_lo_kernel(tc, xT, gate, w1, offs, out_0, out_1, 
             stage(nc.scalar.copy, t, T - CHUNK, T)
         for c0, c1 in ((0, 2 * CHUNK), (2 * CHUNK, T - CHUNK)):
             stage(nc.vector.tensor_copy, last, c0, c1)
-        for c0 in (0, CHUNK, 3 * CHUNK, 2 * CHUNK):
+        for c0 in range(0, T, CHUNK):
             weave_words(c0 < 2 * CHUNK, c0)
 
         out_codes = keep.tile([P, T], U32, name="out_codes", align_bytes=64)
         out_scales = keep.tile([P, T], U8, name="out_scales", align_bytes=64)
         words = out_1[0].rearrange("p c r -> p (c r)").bitcast(I32)
-        for c0 in (0, CHUNK, 3 * CHUNK, 2 * CHUNK):
+        for c0 in range(0, T, CHUNK):
             c1 = c0 + CHUNK
             nc.vector.quantize_mx(
                 out=out_codes[:, c0:c1].bitcast(FP8X4), scales=out_scales[:, c0:c1], in_=grouped[:, PACK * c0 : PACK * c1]

@@ -219,11 +219,12 @@ def tile_picked_modgate_linnone_lo_kernel(tc, xT, gate, w1, offs, out_0, out_1, 
             nc.vector.quantize_mx(
                 out=out_codes[:, c0:c1].bitcast(FP8X4), scales=out_scales[:, c0:c1], in_=grouped[:, PACK * c0 : PACK * c1]
             )
-            if c0 > 0:
+            if 0 < c0 < T - CHUNK:
                 first = 0 if c0 == CHUNK else c0
                 nc.sync.dma_start(words[:, first:c1], out_codes[:, first:c1].bitcast(I32))
-        for q in range(4):
-            queue = nc.sync if q < 2 else nc.scalar
+        for q in (0, 2, 1, 3):
+            queue = nc.sync if q == 0 else nc.scalar
             queue.dma_start(
                 out_2[0, 4 * q : 4 * q + 4, :].bitcast(I32), out_scales[32 * q : 32 * q + 4, :].bitcast(I32)
             )
+        nc.sync.dma_start(words[:, T - CHUNK :], out_codes[:, T - CHUNK :].bitcast(I32))

@@ -50,15 +50,14 @@ def tile_picked_modgate_linnone_lo_kernel(tc, xT, gate, w1, offs, out_0, out_1, 
 
         zero = keep.tile([P, 1], F32, name="zero")
         nc.vector.memset(zero[:], 0.0)
-        nc.scalar.activation(gate_row[:LAST, :CHUNK], zero[:LAST, :].to_broadcast([LAST, CHUNK]), COPY)
-        nc.vector.memset(gate_row[:LAST, CHUNK:], 0.0)
+        nc.scalar.activation(gate_row[:LAST, :LIST_ROWS], zero[:LAST, :].to_broadcast([LAST, LIST_ROWS]), COPY)
+        nc.gpsimd.memset(gate_row[:LAST, LIST_ROWS:], 0.0)
 
         identity = keep.tile([P, P], F32, name="identity")
         make_identity(nc, identity[:])
         windows = [keep.tile([P, T], F32, name=f"window{t}", align_bytes=64) for t in range(PACK)]
         for t in range(PACK):
-            engine = nc.vector if t == 0 else nc.gpsimd
-            engine.memset(windows[t][:], 0.0)
+            nc.gpsimd.memset(windows[t][:], 0.0)
 
         def offs_of(s0, s1):
             return offsets[:, s0 // LIST_ROWS : s1 // LIST_ROWS]
@@ -67,8 +66,8 @@ def tile_picked_modgate_linnone_lo_kernel(tc, xT, gate, w1, offs, out_0, out_1, 
         room = keep.tile([P, PACK * S + SQ], BF16, name="room", align_bytes=64)
         x_picked = room[:, : PACK * S].rearrange("p (j s) -> p j s", j=PACK)
         gate_first = room[:, PAIR * S + SQ :].bitcast(F32)
-        for s0 in (SH, 0):
-            nc.vector.tensor_copy(gate_first[:, s0 : s0 + SH], gate_row[:].indirect(offs_of(s0, s0 + SH)))
+        nc.vector.tensor_copy(gate_first[:, SH:], gate_row[:].indirect(offs_of(SH, S)))
+        nc.scalar.activation(gate_first[:, :SH], gate_row[:].indirect(offs_of(0, SH)), COPY)
         turned = psum.tile([P, blocks, P], F32, name="turned")
         for b in (2, 3, 0, 1):
             nc.tensor.transpose(turned[:, b, :], gate_first[:, P * b : P * (b + 1)], identity[:])

@@ -26,6 +26,7 @@ SH = S // 2
 SQ = S // 4
 CHUNK = 256
 GIVEN = 160
+EARLY = T - 96
 LAST = P - 1
 
 
@@ -148,7 +149,7 @@ def tile_picked_modgate_linnone_lo_kernel(tc, xT, gate, w1, offs, out_0, out_1, 
         room_out = keep.tile([P, PAIR * T + SQ], F32, name="room_out", align_bytes=64)
         paired = room_out[:, : PAIR * T]
         y = [keep.tile([P, S], F32, name=f"y{t}", align_bytes=64)[:] for t in range(PAIR)]
-        y.extend(room_out[:, c0 : c0 + S] for c0 in (T + SQ, T + SQ + S))
+        y.extend(room_out[:, c0 : c0 + S] for c0 in (EARLY, T + SQ + S))
         pieces = ((0, 0, SQ), (0, SQ, S), (1, 0, S), (2, 0, S), (3, 0, S))
         banks = {}
         for t, s0, s1 in pieces:
@@ -157,8 +158,9 @@ def tile_picked_modgate_linnone_lo_kernel(tc, xT, gate, w1, offs, out_0, out_1, 
             for a0, a1 in zip(cuts, cuts[1:]):
                 product(banks[t, s0][:, a0 - s0 : a1 - s0], t, a0, a1)
 
-        def weigh(t, s0, s1):
-            nc.vector.tensor_tensor(y[t][:, s0:s1], banks[t, s0], gate_picked[:, s0:s1], MULT)
+        def weigh(t, s0, s1, first=None):
+            first = s0 if first is None else first
+            nc.vector.tensor_tensor(y[t][:, s0:s1], banks[t, first][:, s0 - first : s1 - first], gate_picked[:, s0:s1], MULT)
 
         def scatter(on_vector, t, s0, s1):
             window = windows[t][:].indirect(offs_of(s0, s1))
@@ -173,24 +175,28 @@ def tile_picked_modgate_linnone_lo_kernel(tc, xT, gate, w1, offs, out_0, out_1, 
 
         def finish_early(t):
             nc.sync.dma_start(out_rows[:, t, :], windows[t][:])
-            nc.gpsimd.tensor_scalar(pairs[:, 0, :, t], windows[t][:], 1.0, -0.0, MULT, ADD)
+            nc.gpsimd.tensor_scalar(pairs[:, 0, :EARLY, t], windows[t][:, :EARLY], 1.0, -0.0, MULT, ADD)
 
-        for piece in pieces:
+        def stage(copy, t, c0, c1):
+            copy(pairs[:, t // PAIR, c0:c1, t % PAIR], windows[t][:, c0:c1])
+
+        for piece in pieces[:-1]:
             weigh(*piece)
+        weigh(last, 0, SH)
         scatter(False, 0, 0, SQ)
         scatter(False, 0, SQ, S)
         finish_early(0)
         scatter(True, 1, 0, S)
         finish_early(1)
+        weigh(last, SH, S, 0)
         scatter(False, 2, 0, GIVEN)
         scatter(True, 2, GIVEN, S)
         scatter(False, 3, 0, SH)
+        for t in range(PAIR):
+            stage(nc.scalar.copy, t, EARLY, T)
         scatter(False, 3, SH, S)
         for t in (2, 3):
             nc.sync.dma_start(out_rows[:, t, :], windows[t][:])
-
-        def stage(copy, t, c0, c1):
-            copy(pairs[:, 1, c0:c1, t % PAIR], windows[t][:, c0:c1])
 
         grouped = keep.tile([P, T * PACK], BF16, name="out_grouped", align_bytes=64)
 
@@ -205,7 +211,7 @@ def tile_picked_modgate_linnone_lo_kernel(tc, xT, gate, w1, offs, out_0, out_1, 
         stage(nc.vector.tensor_copy, PAIR, 0, T - CHUNK)
         for t in (PAIR, last):
             stage(nc.scalar.copy, t, T - CHUNK, T)
-        for c0, c1 in ((0, 2 * CHUNK), (2 * CHUNK, T - CHUNK)):
+        for c0, c1 in ((0, CHUNK), (CHUNK, T - CHUNK)):
             stage(nc.vector.tensor_copy, last, c0, c1)
         for c0 in range(0, T, CHUNK):
             weave_words(c0 < 2 * CHUNK, c0)

@@ -25,8 +25,7 @@ LIST_ROWS = 16
 SH = S // 2
 SQ = S // 4
 CHUNK = 256
-GIVEN = 160
-EARLY = T - 96
+GIVEN = 192
 LAST = P - 1
 
 
@@ -51,6 +50,8 @@ def tile_picked_modgate_linnone_lo_kernel(tc, xT, gate, w1, offs, out_0, out_1, 
 
         zero = keep.tile([P, 1], F32, name="zero")
         nc.vector.memset(zero[:], 0.0)
+        one = keep.tile([P, 1], F32, name="one")
+        nc.vector.memset(one[:], 1.0)
         nc.scalar.activation(gate_row[:LAST, :LIST_ROWS], zero[:LAST, :].to_broadcast([LAST, LIST_ROWS]), COPY)
         nc.gpsimd.memset(gate_row[:LAST, LIST_ROWS:], 0.0)
 
@@ -146,10 +147,10 @@ def tile_picked_modgate_linnone_lo_kernel(tc, xT, gate, w1, offs, out_0, out_1, 
                 stop=True,
             )
 
-        room_out = keep.tile([P, PAIR * T + SQ], F32, name="room_out", align_bytes=64)
+        room_out = keep.tile([P, PAIR * T + CHUNK], F32, name="room_out", align_bytes=64)
         paired = room_out[:, : PAIR * T]
-        y = [keep.tile([P, S], F32, name=f"y{t}", align_bytes=64)[:] for t in range(PAIR)]
-        y.extend(room_out[:, c0 : c0 + S] for c0 in (EARLY, T + SQ + S))
+        y = [keep.tile([P, S], F32, name=f"y{t}", align_bytes=64)[:] for t in range(last)]
+        y.append(room_out[:, PAIR * T - CHUNK :])
         pieces = ((0, 0, SQ), (0, SQ, S), (1, 0, S), (2, 0, S), (3, 0, S))
         banks = {}
         for t, s0, s1 in pieces:
@@ -158,14 +159,15 @@ def tile_picked_modgate_linnone_lo_kernel(tc, xT, gate, w1, offs, out_0, out_1, 
             for a0, a1 in zip(cuts, cuts[1:]):
                 product(banks[t, s0][:, a0 - s0 : a1 - s0], t, a0, a1)
 
-        def weigh(t, s0, s1, first=None):
-            first = s0 if first is None else first
-            nc.vector.tensor_tensor(y[t][:, s0:s1], banks[t, first][:, s0 - first : s1 - first], gate_picked[:, s0:s1], MULT)
+        def weigh(t, s0, s1):
+            nc.vector.tensor_tensor(y[t][:, s0:s1], banks[t, s0], gate_picked[:, s0:s1], MULT)
 
         def scatter(on_vector, t, s0, s1):
             window = windows[t][:].indirect(offs_of(s0, s1))
             if on_vector:
                 nc.vector.tensor_copy(window, y[t][:, s0:s1])
+            elif s1 - s0 == S:
+                nc.scalar.activation(window, y[t][:, s0:s1], COPY, scale=one[:])
             else:
                 nc.scalar.activation(window, y[t][:, s0:s1], COPY)
 
@@ -175,26 +177,21 @@ def tile_picked_modgate_linnone_lo_kernel(tc, xT, gate, w1, offs, out_0, out_1, 
 
         def finish_early(t):
             nc.sync.dma_start(out_rows[:, t, :], windows[t][:])
-            nc.gpsimd.tensor_scalar(pairs[:, 0, :EARLY, t], windows[t][:, :EARLY], 1.0, -0.0, MULT, ADD)
+            nc.gpsimd.tensor_scalar(pairs[:, 0, :, t], windows[t][:], 1.0, -0.0, MULT, ADD)
 
         def stage(copy, t, c0, c1):
             copy(pairs[:, t // PAIR, c0:c1, t % PAIR], windows[t][:, c0:c1])
 
-        for piece in pieces[:-1]:
+        for piece in pieces:
             weigh(*piece)
-        weigh(last, 0, SH)
         scatter(False, 0, 0, SQ)
         scatter(False, 0, SQ, S)
         finish_early(0)
+        scatter(False, 2, 0, GIVEN)
+        scatter(False, last, 0, S)
         scatter(True, 1, 0, S)
         finish_early(1)
-        weigh(last, SH, S, 0)
-        scatter(False, 2, 0, GIVEN)
         scatter(True, 2, GIVEN, S)
-        scatter(False, 3, 0, SH)
-        for t in range(PAIR):
-            stage(nc.scalar.copy, t, EARLY, T)
-        scatter(False, 3, SH, S)
         for t in (2, 3):
             nc.sync.dma_start(out_rows[:, t, :], windows[t][:])
 

@@ -27,6 +27,7 @@ SQ = S // 4
 CHUNK = 256
 GIVEN = 192
 LAST = P - 1
+DMA_ALIGN = 256
 
 
 def tile_picked_modgate_linnone_lo_kernel(tc, xT, gate, w1, offs, out_0, out_1, out_2):
@@ -35,11 +36,11 @@ def tile_picked_modgate_linnone_lo_kernel(tc, xT, gate, w1, offs, out_0, out_1, 
         keep = ctx.enter_context(tc.tile_pool(name="keep", bufs=1))
         psum = ctx.enter_context(tc.psum_pool(name="psum", bufs=1))
 
-        gate_row = keep.tile([P, T], F32, name="gate_row", align_bytes=64)
+        gate_row = keep.tile([P, T], F32, name="gate_row", align_bytes=DMA_ALIGN)
         offsets = keep.tile([P, S // LIST_ROWS], U16, name="offsets")
         x_rows = xT.rearrange("(p j) c -> p j c", j=PACK)
-        x_raw = [keep.tile([P, T], F32, name=f"x_raw{j}", align_bytes=64) for j in range(PACK)]
-        w_raw = keep.tile([P, PACK, N], F32, name="w_raw", align_bytes=64)
+        x_raw = [keep.tile([P, T], F32, name=f"x_raw{j}", align_bytes=DMA_ALIGN) for j in range(PACK)]
+        w_raw = keep.tile([P, PACK, N], F32, name="w_raw", align_bytes=DMA_ALIGN)
         nc.scalar.dma_start(gate_row[LAST:, :], gate[0:1, :])
         nc.sync.dma_start(x_raw[0][:, :CHUNK], x_rows[:, 0, :CHUNK])
         nc.sync.dma_start(offsets[:], offs)
@@ -57,7 +58,7 @@ def tile_picked_modgate_linnone_lo_kernel(tc, xT, gate, w1, offs, out_0, out_1, 
 
         identity = keep.tile([P, P], F32, name="identity")
         make_identity(nc, identity[:])
-        windows = [keep.tile([P, T], F32, name=f"window{t}", align_bytes=64) for t in range(PACK)]
+        windows = [keep.tile([P, T], F32, name=f"window{t}", align_bytes=DMA_ALIGN) for t in range(PACK)]
         for t in range(PACK):
             nc.gpsimd.memset(windows[t][:], 0.0)
 
@@ -213,8 +214,8 @@ def tile_picked_modgate_linnone_lo_kernel(tc, xT, gate, w1, offs, out_0, out_1, 
         for c0 in range(0, T, CHUNK):
             weave_words(c0 < 2 * CHUNK, c0)
 
-        out_codes = keep.tile([P, T], U32, name="out_codes", align_bytes=64)
-        out_scales = keep.tile([P, T], U8, name="out_scales", align_bytes=64)
+        out_codes = keep.tile([P, T], U32, name="out_codes", align_bytes=DMA_ALIGN)
+        out_scales = keep.tile([P, T], U8, name="out_scales", align_bytes=DMA_ALIGN)
         words = out_1[0].rearrange("p c r -> p (c r)").bitcast(I32)
         for c0 in range(0, T, CHUNK):
             c1 = c0 + CHUNK

@@ -26,6 +26,7 @@ SH = S // 2
 SQ = S // 4
 CHUNK = 256
 GIVEN = 192
+EARLY = T - 128
 LAST = P - 1
 DMA_ALIGN = 256
 
@@ -150,8 +151,9 @@ def tile_picked_modgate_linnone_lo_kernel(tc, xT, gate, w1, offs, out_0, out_1, 
 
         room_out = keep.tile([P, PAIR * T + CHUNK], F32, name="room_out", align_bytes=64)
         paired = room_out[:, : PAIR * T]
-        y = [keep.tile([P, S], F32, name=f"y{t}", align_bytes=64)[:] for t in range(last)]
-        y.append(room_out[:, PAIR * T - CHUNK :])
+        y = {t: keep.tile([P, S], F32, name=f"y{t}", align_bytes=64)[:] for t in (0, PAIR)}
+        y[1] = room_out[:, EARLY : EARLY + S]
+        y[last] = room_out[:, PAIR * T - CHUNK :]
         pieces = ((0, 0, SQ), (0, SQ, S), (1, 0, S), (2, 0, S), (3, 0, S))
         banks = {}
         for t, s0, s1 in pieces:
@@ -178,7 +180,7 @@ def tile_picked_modgate_linnone_lo_kernel(tc, xT, gate, w1, offs, out_0, out_1, 
 
         def finish_early(t):
             nc.sync.dma_start(out_rows[:, t, :], windows[t][:])
-            nc.gpsimd.tensor_scalar(pairs[:, 0, :, t], windows[t][:], 1.0, -0.0, MULT, ADD)
+            nc.gpsimd.tensor_scalar(pairs[:, 0, :EARLY, t], windows[t][:, :EARLY], 1.0, -0.0, MULT, ADD)
 
         def stage(copy, t, c0, c1):
             copy(pairs[:, t // PAIR, c0:c1, t % PAIR], windows[t][:, c0:c1])
@@ -193,14 +195,16 @@ def tile_picked_modgate_linnone_lo_kernel(tc, xT, gate, w1, offs, out_0, out_1, 
         scatter(True, 1, 0, S)
         finish_early(1)
         scatter(True, 2, GIVEN, S)
+        for t in range(PAIR):
+            stage(nc.vector.tensor_copy, t, EARLY, T)
         for t in (2, 3):
             nc.sync.dma_start(out_rows[:, t, :], windows[t][:])
 
         grouped = keep.tile([P, T * PACK], BF16, name="out_grouped", align_bytes=64)
 
-        def weave_words(on_vector, c0):
-            dst = grouped[:, PACK * c0 : PACK * (c0 + CHUNK)].bitcast(U32).rearrange("p (c i u) -> p c u i", i=LINE, u=PAIR)
-            src = pair_words[:, :, c0 : c0 + CHUNK].rearrange("p u (c i) -> p c u i", i=LINE)
+        def weave_words(on_vector, c0, c1):
+            dst = grouped[:, PACK * c0 : PACK * c1].bitcast(U32).rearrange("p (c i u) -> p c u i", i=LINE, u=PAIR)
+            src = pair_words[:, :, c0:c1].rearrange("p u (c i) -> p c u i", i=LINE)
             if on_vector:
                 nc.vector.tensor_copy(dst.bitcast(I32), src.bitcast(I32))
             else:
@@ -211,23 +215,24 @@ def tile_picked_modgate_linnone_lo_kernel(tc, xT, gate, w1, offs, out_0, out_1, 
             stage(nc.scalar.copy, t, T - CHUNK, T)
         for c0, c1 in ((0, CHUNK), (CHUNK, T - CHUNK)):
             stage(nc.vector.tensor_copy, last, c0, c1)
-        for c0 in range(0, T, CHUNK):
-            weave_words(c0 < 2 * CHUNK, c0)
+        cuts = list(range(0, T, CHUNK)) + [T - CHUNK // 2, T]
+        for c0, c1 in zip(cuts, cuts[1:]):
+            weave_words(c0 < 2 * CHUNK, c0, c1)
 
         out_codes = keep.tile([P, T], U32, name="out_codes", align_bytes=DMA_ALIGN)
         out_scales = keep.tile([P, T], U8, name="out_scales", align_bytes=DMA_ALIGN)
         words = out_1[0].rearrange("p c r -> p (c r)").bitcast(I32)
-        for c0 in range(0, T, CHUNK):
-            c1 = c0 + CHUNK
+        stored = 0
+        for c0, c1 in zip(cuts, cuts[1:]):
             nc.vector.quantize_mx(
                 out=out_codes[:, c0:c1].bitcast(FP8X4), scales=out_scales[:, c0:c1], in_=grouped[:, PACK * c0 : PACK * c1]
             )
-            if 0 < c0 < T - CHUNK:
-                first = 0 if c0 == CHUNK else c0
-                nc.sync.dma_start(words[:, first:c1], out_codes[:, first:c1].bitcast(I32))
+            if c1 in (T // 2, cuts[-2]):
+                nc.sync.dma_start(words[:, stored:c1], out_codes[:, stored:c1].bitcast(I32))
+                stored = c1
         for q in (0, 2, 1, 3):
             queue = nc.sync if q == 0 else nc.scalar
             queue.dma_start(
                 out_2[0, 4 * q : 4 * q + 4, :].bitcast(I32), out_scales[32 * q : 32 * q + 4, :].bitcast(I32)
             )
-        nc.sync.dma_start(words[:, T - CHUNK :], out_codes[:, T - CHUNK :].bitcast(I32))
+        nc.sync.dma_start(words[:, stored:], out_codes[:, stored:].bitcast(I32))

@@ -26,7 +26,6 @@ SH = S // 2
 SQ = S // 4
 CHUNK = 256
 GIVEN = 192
-EARLY = T - 128
 LAST = P - 1
 DMA_ALIGN = 256
 
@@ -151,9 +150,8 @@ def tile_picked_modgate_linnone_lo_kernel(tc, xT, gate, w1, offs, out_0, out_1, 
 
         room_out = keep.tile([P, PAIR * T + CHUNK], F32, name="room_out", align_bytes=64)
         paired = room_out[:, : PAIR * T]
-        y = {t: keep.tile([P, S], F32, name=f"y{t}", align_bytes=64)[:] for t in (0, PAIR)}
-        y[1] = room_out[:, EARLY : EARLY + S]
-        y[last] = room_out[:, PAIR * T - CHUNK :]
+        y = [keep.tile([P, S], F32, name=f"y{t}", align_bytes=64)[:] for t in range(last)]
+        y.append(room_out[:, PAIR * T - CHUNK :])
         pieces = ((0, 0, SQ), (0, SQ, S), (1, 0, S), (2, 0, S), (3, 0, S))
         banks = {}
         for t, s0, s1 in pieces:
@@ -180,7 +178,7 @@ def tile_picked_modgate_linnone_lo_kernel(tc, xT, gate, w1, offs, out_0, out_1, 
 
         def finish_early(t):
             nc.sync.dma_start(out_rows[:, t, :], windows[t][:])
-            nc.gpsimd.tensor_scalar(pairs[:, 0, :EARLY, t], windows[t][:, :EARLY], 1.0, -0.0, MULT, ADD)
+            nc.gpsimd.tensor_scalar(pairs[:, 0, :, t], windows[t][:], 1.0, -0.0, MULT, ADD)
 
         def stage(copy, t, c0, c1):
             copy(pairs[:, t // PAIR, c0:c1, t % PAIR], windows[t][:, c0:c1])
@@ -195,8 +193,6 @@ def tile_picked_modgate_linnone_lo_kernel(tc, xT, gate, w1, offs, out_0, out_1, 
         scatter(True, 1, 0, S)
         finish_early(1)
         scatter(True, 2, GIVEN, S)
-        for t in range(PAIR):
-            stage(nc.vector.tensor_copy, t, EARLY, T)
         for t in (2, 3):
             nc.sync.dma_start(out_rows[:, t, :], windows[t][:])
 
@@ -227,7 +223,7 @@ def tile_picked_modgate_linnone_lo_kernel(tc, xT, gate, w1, offs, out_0, out_1, 
             nc.vector.quantize_mx(
                 out=out_codes[:, c0:c1].bitcast(FP8X4), scales=out_scales[:, c0:c1], in_=grouped[:, PACK * c0 : PACK * c1]
             )
-            if c1 in (T // 2, cuts[-2]):
+            if c1 in (T // 2, T - CHUNK):
                 nc.sync.dma_start(words[:, stored:c1], out_codes[:, stored:c1].bitcast(I32))
                 stored = c1
         for q in (0, 2, 1, 3):

@@ -42,9 +42,9 @@ def tile_picked_modgate_linnone_lo_kernel(tc, xT, gate, w1, offs, out_0, out_1, 
         x_raw = [keep.tile([P, T], F32, name=f"x_raw{j}", align_bytes=DMA_ALIGN) for j in range(PACK)]
         w_raw = keep.tile([P, PACK, N], F32, name="w_raw", align_bytes=DMA_ALIGN)
         nc.scalar.dma_start(gate_row[LAST:, :], gate[0:1, :])
-        nc.sync.dma_start(x_raw[0][:, :CHUNK], x_rows[:, 0, :CHUNK])
+        nc.sync.dma_start(x_raw[0][:, : T // 2], x_rows[:, 0, : T // 2])
         nc.sync.dma_start(offsets[:], offs)
-        nc.sync.dma_start(x_raw[0][:, CHUNK:], x_rows[:, 0, CHUNK:])
+        nc.sync.dma_start(x_raw[0][:, T // 2 :], x_rows[:, 0, T // 2 :])
         for j in range(1, PACK):
             nc.sync.dma_start(x_raw[j][:], x_rows[:, j, :])
         nc.sync.dma_start(w_raw[:], w1.rearrange("(p j) c -> p j c", j=PACK))

from contextlib import ExitStack

import concourse.mybir as mybir
from concourse.masks import make_identity

K, T, S, N = 512, 1024, 512, 512
FLOPS = 2 * K * N * S

F32 = mybir.dt.float32
BF16 = mybir.dt.bfloat16
U32 = mybir.dt.uint32
I32 = mybir.dt.int32
U16 = mybir.dt.uint16
U8 = mybir.dt.uint8
FP8X4 = mybir.dt.float8_e4m3fn_x4
COPY = mybir.ActivationFunctionType.Copy
MULT = mybir.AluOpType.mult
ADD = mybir.AluOpType.add

P = 128
PACK = 4
PAIR = 2
LINE = 4
LIST_ROWS = 16
SH = S // 2
SQ = S // 4
CHUNK = 256
GIVEN = 192
LAST = P - 1
DMA_ALIGN = 256


def tile_picked_modgate_linnone_lo_kernel(tc, xT, gate, w1, offs, out_0, out_1, out_2):
    nc = tc.nc
    with ExitStack() as ctx:
        keep = ctx.enter_context(tc.tile_pool(name="keep", bufs=1))
        psum = ctx.enter_context(tc.psum_pool(name="psum", bufs=1))

        gate_row = keep.tile([P, T], F32, name="gate_row", align_bytes=DMA_ALIGN)
        offsets = keep.tile([P, S // LIST_ROWS], U16, name="offsets")
        x_rows = xT.rearrange("(p j) c -> p j c", j=PACK)
        x_raw = [keep.tile([P, T], F32, name=f"x_raw{j}", align_bytes=DMA_ALIGN) for j in range(PACK)]
        w_raw = keep.tile([P, PACK, N], F32, name="w_raw", align_bytes=DMA_ALIGN)
        nc.scalar.dma_start(gate_row[LAST:, :], gate[0:1, :])
        nc.sync.dma_start(x_raw[0][:, : T // 2], x_rows[:, 0, : T // 2])
        nc.sync.dma_start(offsets[:], offs)
        nc.sync.dma_start(x_raw[0][:, T // 2 :], x_rows[:, 0, T // 2 :])
        for j in range(1, PACK):
            nc.sync.dma_start(x_raw[j][:], x_rows[:, j, :])
        nc.sync.dma_start(w_raw[:], w1.rearrange("(p j) c -> p j c", j=PACK))

        zero = keep.tile([P, 1], F32, name="zero")
        nc.vector.memset(zero[:], 0.0)
        one = keep.tile([P, 1], F32, name="one")
        nc.vector.memset(one[:], 1.0)
        nc.scalar.activation(gate_row[:LAST, :LIST_ROWS], zero[:LAST, :].to_broadcast([LAST, LIST_ROWS]), COPY)
        nc.gpsimd.memset(gate_row[:LAST, LIST_ROWS:], 0.0)

        identity = keep.tile([P, P], F32, name="identity")
        make_identity(nc, identity[:])
        windows = [keep.tile([P, T], F32, name=f"window{t}", align_bytes=DMA_ALIGN) for t in range(PACK)]
        for t in range(PACK):
            nc.gpsimd.memset(windows[t][:], 0.0)

        def offs_of(s0, s1):
            return offsets[:, s0 // LIST_ROWS : s1 // LIST_ROWS]

        blocks = S // P
        room = keep.tile([P, PACK * S + SQ], BF16, name="room", align_bytes=64)
        x_picked = room[:, : PACK * S].rearrange("p (j s) -> p j s", j=PACK)
        gate_first = room[:, PAIR * S + SQ :].bitcast(F32)
        nc.vector.tensor_copy(gate_first[:, SH:], gate_row[:].indirect(offs_of(SH, S)))
        nc.scalar.activation(gate_first[:, :SH], gate_row[:].indirect(offs_of(0, SH)), COPY)
        turned = psum.tile([P, blocks, P], F32, name="turned")
        for b in (2, 3, 0, 1):
            nc.tensor.transpose(turned[:, b, :], gate_first[:, P * b : P * (b + 1)], identity[:])
        gate_column = keep.tile([P, blocks], F32, name="gate_column")
        nc.vector.tensor_copy(gate_column[:], turned[:, :, LAST])
        spread = psum.tile([P, blocks, P], F32, name="spread")
        for b in range(blocks):
            nc.tensor.transpose(spread[:, b, :], gate_column[:, b : b + 1].to_broadcast([P, P]), identity[:])

        last = PACK - 1

        def gather(on_vector, j, s0, s1):
            picked = x_raw[j][:].indirect(offs_of(s0, s1))
            if on_vector:
                nc.vector.tensor_copy(x_picked[:, j, s0:s1], picked)
            else:
                nc.scalar.activation(x_picked[:, j, s0:s1], picked, COPY)

        for j in range(PAIR):
            gather(False, j, 0, S)
        gather(False, PAIR, 0, SQ)
        gather(True, PAIR, SQ, S)
        gather(True, last, 0, SQ)
        for s0 in range(SQ, S, SQ):
            gather(False, last, s0, s0 + SQ)

        def weave(copy, dst, src):
            copy(
                dst.rearrange("p (c i t) -> p c t i", i=LINE, t=PACK),
                src.rearrange("p t (c i) -> p c t i", i=LINE),
            )

        x_grouped = keep.tile([P, S * PACK], BF16, name="x_grouped", align_bytes=64)
        x_codes = keep.tile([P, S], U32, name="x_codes", align_bytes=64)
        x_scales = keep.tile([P, S], U8, name="x_scales", align_bytes=64)
        for q in (1, 0, 2, 3):
            copy = nc.scalar.copy if q == 3 else nc.vector.tensor_copy
            weave(copy, x_grouped[:, PACK * SQ * q : PACK * SQ * (q + 1)], x_picked[:, :, SQ * q : SQ * (q + 1)])

        def quantise_x(s0, s1):
            nc.vector.quantize_mx(
                out=x_codes[:, s0:s1].bitcast(FP8X4), scales=x_scales[:, s0:s1], in_=x_grouped[:, PACK * s0 : PACK * s1]
            )

        quantise_x(0, SH)
        quantise_x(SH, S - SQ)

        gate_picked = keep.tile([P, S], F32, name="gate_picked", align_bytes=64)
        nc.scalar.copy(gate_picked[:], spread[:].rearrange("p b n -> p (b n)"))

        w_src = w_raw[:].rearrange("p j (m t) -> p m j t", t=PACK)
        w_codes = [keep.tile([P, PAIR * P], U32, name=f"w_codes{h}", align_bytes=64) for h in range(2)]
        w_scales = [keep.tile([P, PAIR * P], U8, name=f"w_scales{h}", align_bytes=64) for h in range(2)]
        w_dealt = [x_picked[:, PAIR * h : PAIR * (h + 1), :] for h in range(2)]
        for h, copy in enumerate((nc.vector.tensor_copy, nc.scalar.copy)):
            copy(w_dealt[h].rearrange("p t (m j) -> p m j t", j=PACK), w_src[:, :, :, PAIR * h : PAIR * (h + 1)])
        quantise_x(S - SQ, S)

        def quantise_w(h, c0, c1, grouped_w):
            nc.vector.quantize_mx(out=w_codes[h][:, c0:c1].bitcast(FP8X4), scales=w_scales[h][:, c0:c1], in_=grouped_w)

        for t in range(PAIR):
            quantise_w(0, P * t, P * (t + 1), w_dealt[0][:, t, :])
        quantise_w(1, 0, P * PAIR, w_dealt[1].rearrange("p t c -> p (t c)"))

        def product(acc, t, s0, s1):
            h, m0 = t // PAIR, P * (t % PAIR)
            nc.tensor.matmul_mx(
                out=acc,
                lhsT=w_codes[h][:, m0 : m0 + P].bitcast(FP8X4),
                lhsT_scale=w_scales[h][:, m0 : m0 + P],
                rhs=x_codes[:, s0:s1].bitcast(FP8X4),
                rhs_scale=x_scales[:, s0:s1],
                start=True,
                stop=True,
            )

        room_out = keep.tile([P, PAIR * T + CHUNK], F32, name="room_out", align_bytes=64)
        paired = room_out[:, : PAIR * T]
        y = [keep.tile([P, S], F32, name=f"y{t}", align_bytes=64)[:] for t in range(last)]
        y.append(room_out[:, PAIR * T - CHUNK :])
        pieces = ((0, 0, SQ), (0, SQ, S), (1, 0, S), (2, 0, S), (3, 0, S))
        banks = {}
        for t, s0, s1 in pieces:
            banks[t, s0] = psum.tile([P, S], F32, name=f"acc{t}_{s0}")[:, : s1 - s0]
            cuts = (SQ, SH, S) if s0 == SQ else (s0, s1)
            for a0, a1 in zip(cuts, cuts[1:]):
                product(banks[t, s0][:, a0 - s0 : a1 - s0], t, a0, a1)

        def weigh(t, s0, s1):
            nc.vector.tensor_tensor(y[t][:, s0:s1], banks[t, s0], gate_picked[:, s0:s1], MULT)

        def scatter(on_vector, t, s0, s1):
            window = windows[t][:].indirect(offs_of(s0, s1))
            if on_vector:
                nc.vector.tensor_copy(window, y[t][:, s0:s1])
            elif s1 - s0 == S:
                nc.scalar.activation(window, y[t][:, s0:s1], COPY, scale=one[:])
            else:
                nc.scalar.activation(window, y[t][:, s0:s1], COPY)

        out_rows = out_0.rearrange("(p t) c -> p t c", t=PACK)
        pairs = paired.bitcast(BF16).rearrange("p (u c e) -> p u c e", u=PAIR, e=PAIR)
        pair_words = paired.bitcast(U32).rearrange("p (u c) -> p u c", u=PAIR)

        def finish_early(t):
            nc.sync.dma_start(out_rows[:, t, :], windows[t][:])
            nc.gpsimd.tensor_scalar(pairs[:, 0, :, t], windows[t][:], 1.0, -0.0, MULT, ADD)

        def stage(copy, t, c0, c1):
            copy(pairs[:, t // PAIR, c0:c1, t % PAIR], windows[t][:, c0:c1])

        for piece in pieces:
            weigh(*piece)
        scatter(False, 0, 0, SQ)
        scatter(False, 0, SQ, S)
        finish_early(0)
        scatter(False, 2, 0, GIVEN)
        scatter(False, last, 0, S)
        scatter(True, 1, 0, S)
        finish_early(1)
        scatter(True, 2, GIVEN, S)
        for t in (2, 3):
            nc.sync.dma_start(out_rows[:, t, :], windows[t][:])

        grouped = keep.tile([P, T * PACK], BF16, name="out_grouped", align_bytes=64)

        def weave_words(on_vector, c0, c1):
            dst = grouped[:, PACK * c0 : PACK * c1].bitcast(U32).rearrange("p (c i u) -> p c u i", i=LINE, u=PAIR)
            src = pair_words[:, :, c0:c1].rearrange("p u (c i) -> p c u i", i=LINE)
            if on_vector:
                nc.vector.tensor_copy(dst.bitcast(I32), src.bitcast(I32))
            else:
                nc.scalar.copy(dst, src)

        stage(nc.vector.tensor_copy, PAIR, 0, T - CHUNK)
        for t in (PAIR, last):
            stage(nc.scalar.copy, t, T - CHUNK, T)
        for c0, c1 in ((0, CHUNK), (CHUNK, T - CHUNK)):
            stage(nc.vector.tensor_copy, last, c0, c1)
        cuts = list(range(0, T, CHUNK)) + [T - CHUNK // 2, T]
        for c0, c1 in zip(cuts, cuts[1:]):
            weave_words(c0 < 2 * CHUNK, c0, c1)

        out_codes = keep.tile([P, T], U32, name="out_codes", align_bytes=DMA_ALIGN)
        out_scales = keep.tile([P, T], U8, name="out_scales", align_bytes=DMA_ALIGN)
        words = out_1[0].rearrange("p c r -> p (c r)").bitcast(I32)
        stored = 0
        for c0, c1 in zip(cuts, cuts[1:]):
            nc.vector.quantize_mx(
                out=out_codes[:, c0:c1].bitcast(FP8X4), scales=out_scales[:, c0:c1], in_=grouped[:, PACK * c0 : PACK * c1]
            )
            if c1 in (T // 2, T - CHUNK):
                nc.sync.dma_start(words[:, stored:c1], out_codes[:, stored:c1].bitcast(I32))
                stored = c1
        for q in (0, 2, 1, 3):
            queue = nc.sync if q == 0 else nc.scalar
            queue.dma_start(
                out_2[0, 4 * q : 4 * q + 4, :].bitcast(I32), out_scales[32 * q : 32 * q + 4, :].bitcast(I32)
            )
        nc.sync.dma_start(words[:, stored:], out_codes[:, stored:].bitcast(I32))
